import numpy as np
import ml_dtypes


def mxq(x, axis, fmt="e4m3"):
    dtype, down = {"e4m3": (ml_dtypes.float8_e4m3fn, 7), "e5m2": (ml_dtypes.float8_e5m2, 14)}[fmt]
    v = np.moveaxis(np.asarray(x, np.float32).astype(ml_dtypes.bfloat16).astype(np.float64), axis, -1)
    blocks = v.reshape(v.shape[:-1] + (-1, 32))
    amax = np.abs(blocks).max(-1, keepdims=True)
    byte = np.maximum(np.where(amax > 0, np.frexp(amax)[1] - 1 + 127, 0) - down, 1)
    scale = np.exp2(byte - 127.0)
    codes = (blocks / scale).astype(np.float32).astype(dtype).astype(np.float64)
    return np.moveaxis((codes * scale).reshape(v.shape), -1, axis)


WIDE = False


def mx_kscale(k):
    if not WIDE:
        return np.ones(k)
    levels = np.array([10, -10, 5, -5, 0])
    if k % 512:
        return np.exp2(np.random.permutation(np.resize(levels, k // 32))).repeat(32)
    a = np.empty((k // 512, 16))
    for p in range(k // 512):
        a[p, :8] = np.random.permutation(np.resize(levels, 8))
        for g in range(8):
            far = levels[np.abs(levels - a[p, g]) >= 10]
            a[p, g + 8] = far[np.random.randint(len(far))]
    return np.exp2(a.ravel()).repeat(32)


BF16 = ml_dtypes.bfloat16


def bf(x):
    return np.asarray(x, np.float32).astype(BF16)


def f64(x):
    return np.asarray(x).astype(np.float64)


E2M1 = np.array([0.0, 0.5, 1.0, 1.5, 2.0, 3.0, 4.0, 6.0, -0.0, -0.5, -1.0, -1.5, -2.0, -3.0, -4.0, -6.0])


def pack_weight(w, fmt):
    k, n = w.shape
    w = f64(bf(w)).reshape(k // 32, 32, n)
    amax = np.abs(w).max(1)
    if fmt == "e4m3":
        byte = np.frexp(amax)[1] - 1 + 127 - 7
    else:
        mant, ex = np.frexp(amax / 6.0)
        byte = np.where(mant > 0.5, ex, ex - 1) + 127
    byte = np.clip(np.where(amax > 0, byte, 1), 1, 254)
    scaled = (w * np.exp2(127.0 - byte)[:, None, :]).reshape(k, n).astype(np.float32)
    by_word = np.ascontiguousarray(scaled.reshape(k // 512, 128, 4, n).transpose(0, 1, 3, 2))
    if fmt == "e4m3":
        words = by_word.astype(ml_dtypes.float8_e4m3fn).view(np.uint8)
    else:
        c = by_word.astype(ml_dtypes.float4_e2m1fn).view(np.uint8) & 0xF
        words = c[..., 0::2] | (c[..., 1::2] << 4)
    return np.ascontiguousarray(words), np.ascontiguousarray(byte.astype(np.uint8).reshape(k // 512, 16, n))


def unpack_weight(words, scales, fmt):
    g, p, n, _ = words.shape
    if fmt == "e4m3":
        vals = np.ascontiguousarray(words).view(ml_dtypes.float8_e4m3fn).astype(np.float64)
    else:
        nib = np.empty((g, p, n, 4), np.uint8)
        nib[..., 0::2] = words & 0xF
        nib[..., 1::2] = words >> 4
        vals = E2M1[nib]
    vals = vals * np.repeat(np.exp2(scales.astype(np.float64) - 127.0), 8, axis=1)[..., None]
    return vals.transpose(0, 1, 3, 2).reshape(g * 512, n)


B, N, D, F, O = 2, 64, 512, 512, 512
F2 = 2 * F


def sigmoid(v):
    return 1.0 / (1.0 + np.exp(-v))


def scaled_layer_norm(y, gamma):
    mu = np.mean(y, axis=-1, keepdims=True)
    centered = y - mu
    var = np.mean(centered * centered, axis=-1, keepdims=True)
    return centered / np.sqrt(var + 1e-5) * gamma


def draw0():
    s = mx_kscale(D)
    u = mx_kscale(D)
    t = mx_kscale(F)
    e = np.random.standard_normal((B, N, N, D))
    x = np.random.standard_normal((B, N, D))
    we = np.random.standard_normal((D, F)) / np.sqrt(D)
    wn = np.random.standard_normal((D, F2)) / np.sqrt(D)
    g = 1.0 + 0.1 * np.random.standard_normal(F)
    w2 = 0.015 * (np.random.standard_normal((F, O)) / np.sqrt(F) + 0.5 / F)
    gamma = 1.0 + 0.1 * np.random.standard_normal(O)
    we_words, we_scales = pack_weight(we / s[:, None], "e4m3")
    wn_words, wn_scales = pack_weight(wn / u[:, None], "e4m3")
    w2_words, w2_scales = pack_weight(w2 / t[:, None], "e4m3")
    return {
        "e": bf(e * s),
        "x": bf(x * u),
        "we_words": we_words,
        "we_scales": we_scales,
        "wn_words": wn_words,
        "wn_scales": wn_scales,
        "g": bf(g * t),
        "w2_words": w2_words,
        "w2_scales": w2_scales,
        "gamma": bf(gamma),
    }


def core(e, x, we_words, we_scales, wn_words, wn_scales, g, w2_words, w2_scales, gamma):
    f = we_words.shape[2]

    pe = mxq(f64(e), 3, "e4m3") @ unpack_weight(we_words, we_scales, "e4m3")

    pn = mxq(f64(x), 2, "e4m3") @ unpack_weight(wn_words, wn_scales, "e4m3")
    ps = pn[..., :f]
    pr = pn[..., f:]

    t = pe + ps[:, :, None, :] + pr[:, None, :, :]

    h = t * sigmoid(t) * f64(g)

    y = mxq(h, 3, "e4m3") @ unpack_weight(w2_words, w2_scales, "e4m3")

    return scaled_layer_norm(y, f64(gamma))


def e4m3fn_bytes(y):
    return np.clip(np.asarray(y, np.float64), -448.0, 448.0).astype(np.float32).astype(ml_dtypes.float8_e4m3fn).view(np.uint8)


def e4m3fn_values(b):
    return np.asarray(b, np.uint8).view(ml_dtypes.float8_e4m3fn).astype(np.float64)


def setup_inputs():
    d = draw0()
    x0 = np.asarray(d['e']).astype(np.float64)
    s = (np.max(np.abs(x0), axis=(0, 1, 2), keepdims=True) / 448.0).astype(np.float32)
    out = {}
    for k, v in d.items():
        if k == 'e':
            out['e_bytes'] = e4m3fn_bytes(x0 / s.astype(np.float64))
            out['e_scale'] = s
        else:
            out[k] = v
    return out


def reference(e_bytes, e_scale, x, we_words, we_scales, wn_words, wn_scales, g, w2_words, w2_scales, gamma):
    return core(e4m3fn_values(e_bytes) * e_scale.astype(np.float64), x, we_words, we_scales, wn_words, wn_scales, g, w2_words, w2_scales, gamma)

@@ -1,0 +1,388 @@
+from contextlib import ExitStack
+
+import concourse.mybir as mybir
+from concourse.masks import make_identity
+
+F32 = mybir.dt.float32
+BF16 = mybir.dt.bfloat16
+I32 = mybir.dt.int32
+U32 = mybir.dt.uint32
+U8 = mybir.dt.uint8
+FP8 = mybir.dt.float8_e4m3fn
+FP8X4 = mybir.dt.float8_e4m3fn_x4
+ACT = mybir.ActivationFunctionType
+ALU = mybir.AluOpType
+
+P = 128
+B, N, D, F, O = 2, 64, 512, 512, 512
+ROWS = B * N * N
+CHUNK = 512
+TILES = CHUNK // P
+CHUNKS = ROWS // CHUNK
+CHUNKS_B = CHUNKS // B
+SENDERS = CHUNK // N
+REP = P // SENDERS
+EPS = 1e-5
+
+FLOPS = 2 * ROWS * (D * F + F * O) + 2 * B * N * D * 2 * F
+
+
+def tile_meshgraphnetdenseedgeupdate_w8_kernel(
+    tc, e_bytes, e_scale, x, we_words, we_scales, wn_words, wn_scales, g, w2_words, w2_scales, gamma, out
+):
+    nc = tc.nc
+    e_rows = e_bytes.rearrange("b i j k -> (b i j) k").rearrange("(c p r) k -> c p (r k)", p=P, r=TILES)
+    out_rows = out.rearrange("b i j o -> (b i j) o").rearrange("(c p r) o -> c p (r o)", p=P, r=TILES)
+
+    with ExitStack() as ctx:
+        keep = ctx.enter_context(tc.tile_pool(name="keep", bufs=1))
+        work = ctx.enter_context(tc.tile_pool(name="work", bufs=2))
+        psum = ctx.enter_context(tc.psum_pool(name="psum", bufs=1))
+        ctx.enter_context(tc.manual_schedule())
+
+        ebytes = {}
+
+        def load(c):
+            t = work.tile([P, TILES * D], U8, name="eb", tag="eb", bufs=4, align_bytes=64)
+            nc.sync.dma_start(out=t[:], in_=e_rows[c])
+            ebytes[c] = t
+
+        load(0)
+        xsb = keep.tile([P, D], BF16, name="xsb", align_bytes=64)
+        nc.sync.dma_start(out=xsb[:], in_=x.rearrange("b i k -> (b i) k"))
+        esc = keep.tile([P, 4], F32, name="esc")
+        nc.sync.dma_start(out=esc[:], in_=e_scale.rearrange("a b c (p t) -> p (a b c t)", t=4))
+
+        ident = keep.tile([P, P], F32, name="ident")
+        make_identity(nc, ident[:])
+        mhalf = keep.tile([P, TILES], F32, name="mhalf")
+        nc.gpsimd.memset(mhalf[:], -0.5)
+
+        sraw = keep.tile([P, 2048], U8, name="sraw", align_bytes=64)
+        nc.vector.memset(sraw[:].bitcast(I32), 0)
+        for src, lo, n in ((wn_scales, 512, 1024), (we_scales, 0, 512), (w2_scales, 1536, 512)):
+            view = src[0].rearrange("(q r) n -> r q n", r=4)
+            for r in range(4):
+                nc.sync.dma_start(
+                    out=sraw[r:P:32, lo : lo + n].bitcast(I32), in_=view[r].bitcast(I32)
+                )
+        wraw = keep.tile([P, 1536], I32, name="wraw", align_bytes=64)
+        nc.sync.dma_start(out=wraw[:, 512:1536], in_=wn_words[0].rearrange("p n t -> p (n t)").bitcast(I32))
+        nc.sync.dma_start(out=wraw[:, 0:512], in_=we_words[0].rearrange("p n t -> p (n t)").bitcast(I32))
+        g4 = keep.tile([P, 4], BF16, name="g4")
+        nc.sync.dma_start(out=g4[:], in_=g.rearrange("(p t) -> p t", t=4))
+        load(1)
+        w2w = keep.tile([P, O], I32, name="w2w", align_bytes=64)
+        nc.sync.dma_start(out=w2w[:], in_=w2_words[0].rearrange("p n t -> p (n t)").bitcast(I32))
+        load(2)
+        gam = keep.tile([P, O], BF16, name="gam")
+        nc.sync.dma_start(out=gam[:], in_=gamma.partition_broadcast(P))
+
+        ebf = {}
+
+        def cast(c, h):
+            if h == 0:
+                ebf[c] = work.tile([P, TILES * D], BF16, name="ebf", tag="ebf", align_bytes=64)
+            lo = h * 2 * D
+            nc.scalar.copy(out=ebf[c][:, lo : lo + 2 * D], in_=ebytes[c][:, lo : lo + 2 * D].bitcast(FP8))
+
+        trs = {}
+
+        def turn(c, h):
+            t = psum.tile([P, 2, 2 * P], F32, name="tr", tag="tr", bufs=2)
+            words = ebf[c][:].bitcast(F32)
+            for k in range(2):
+                base = (2 * h + k) * (D // 2)
+                for u in range(2):
+                    nc.tensor.transpose(
+                        t[:, u, k * P : (k + 1) * P], words[:, base + u : base + D // 2 : 2], ident[:]
+                    )
+            trs[c, h] = t
+
+        egr = {}
+
+        def apply_scale(c, h):
+            if h == 0:
+                egr[c] = work.tile([P, CHUNK * 4], BF16, name="egr", tag="egr", align_bytes=64)
+            src = trs[c, h][:].rearrange("p u n -> p (u n)").bitcast(BF16)
+            nc.vector.tensor_tensor(
+                out=egr[c][:, h * 1024 : (h + 1) * 1024].rearrange("p (n u e) -> p n u e", u=2, e=2),
+                in0=src.rearrange("p (u n e) -> p n u e", u=2, e=2),
+                in1=esc[:].rearrange("p (u e) -> p u e", e=2).unsqueeze(1).to_broadcast([P, 256, 2, 2]),
+                op=ALU.mult,
+            )
+
+        ecod, escl = {}, {}
+
+        def quant_e(c, h):
+            if h == 0:
+                ecod[c] = work.tile([P, CHUNK], U32, name="ecod", tag="ecod", align_bytes=64)
+                escl[c] = work.tile([P, CHUNK], U8, name="escl", tag="escl", align_bytes=64)
+            cols = slice(h * 256, (h + 1) * 256)
+            nc.vector.quantize_mx(
+                out=ecod[c][:, cols].bitcast(FP8X4),
+                scales=escl[c][:, cols],
+                in_=egr[c][:, h * 1024 : (h + 1) * 1024],
+            )
+
+        hps, hsil, hg = {}, {}, {}
+
+        def project(c, k):
+            t = psum.tile([P, 4, P], F32, name="hp", tag="hp", bufs=3)
+            cols = slice(k * P, (k + 1) * P)
+            b = c // CHUNKS_B
+            scols = slice((c % 2) * P, (c % 2 + 1) * P)
+            moving = (
+                (rcod[b][:, cols], rscl[b][:, cols], 1024),
+                (scod[c // 2][:, scols], sscl[c // 2][:, scols], 512),
+                (ecod[c][:, cols], escl[c][:, cols], 0),
+            )
+            for j in range(4):
+                for i, (codes, scales, w0) in enumerate(moving):
+                    w = slice(w0 + j * P, w0 + (j + 1) * P)
+                    nc.tensor.matmul_mx(
+                        out=t[:, j, :],
+                        lhsT=wper[:, w].bitcast(FP8X4),
+                        lhsT_scale=sper[:, w],
+                        rhs=codes.bitcast(FP8X4),
+                        rhs_scale=scales,
+                        start=(i == 0),
+                        stop=(i == 2),
+                    )
+            hps[c, k] = t
+
+        def silu(c, k):
+            if k == 0:
+                hsil[c] = work.tile([P, CHUNK * 4], F32, name="hsil", tag="hsil", align_bytes=64)
+            nc.scalar.activation(
+                out=hsil[c][:, k * 512 : (k + 1) * 512].rearrange("p (n t) -> p n t", t=4),
+                in_=hps[c, k][:].rearrange("p t n -> p n t"),
+                func=ACT.Silu,
+            )
+
+        def gain(c, k):
+            if k == 0:
+                hg[c] = work.tile([P, CHUNK * 4], BF16, name="hg", tag="hg", align_bytes=64)
+            cols = slice(k * 512, (k + 1) * 512)
+            nc.gpsimd.tensor_tensor(
+                out=hg[c][:, cols].rearrange("p (n t) -> p n t", t=4),
+                in0=hsil[c][:, cols].rearrange("p (n t) -> p n t", t=4),
+                in1=g4[:].unsqueeze(1).to_broadcast([P, P, 4]),
+                op=ALU.mult,
+            )
+
+        hcod, hscl = {}, {}
+
+        def quant_h(c, h):
+            if h == 0:
+                hcod[c] = work.tile([P, CHUNK], U32, name="hcod", tag="hcod", align_bytes=64)
+                hscl[c] = work.tile([P, CHUNK], U8, name="hscl", tag="hscl", align_bytes=64)
+            cols = slice(h * 256, (h + 1) * 256)
+            nc.vector.quantize_mx(
+                out=hcod[c][:, cols].bitcast(FP8X4),
+                scales=hscl[c][:, cols],
+                in_=hg[c][:, h * 1024 : (h + 1) * 1024],
+            )
+
+        yps, stats, mv, zs, rstd = {}, {}, {}, {}, {}
+
+        def output(c, k):
+            t = psum.tile([P, O], F32, name="yp", tag="yp", bufs=3)
+            cols = slice(k * P, (k + 1) * P)
+            nc.tensor.matmul_mx(
+                out=t[:],
+                lhsT=hcod[c][:, cols].bitcast(FP8X4),
+                lhsT_scale=hscl[c][:, cols],
+                rhs=w2w[:].bitcast(FP8X4),
+                rhs_scale=sraw[:, 1536:2048],
+                start=True,
+                stop=True,
+            )
+            yps[c, k] = t
+
+        def bstats(c, k):
+            if k == 0:
+                stats[c] = work.tile([P, TILES, 6], F32, name="stats", tag="stats", bufs=3)
+                mv[c] = work.tile([P, TILES, 2], F32, name="mv", tag="mv", bufs=3)
+                zs[c] = work.tile([P, TILES, O], F32, name="zs", tag="zs")
+            nc.vector.bn_stats(out=stats[c][:, k, :], in_=yps[c, k][:])
+
+        def baggr(c, k):
+            nc.vector.bn_aggr(out=mv[c][:, k, :], in_=stats[c][:, k, :])
+
+        def center(c, k):
+            nc.vector.scalar_tensor_tensor(
+                out=zs[c][:, k, :],
+                in0=yps[c, k][:],
+                scalar=mv[c][:, k, 0:1],
+                in1=gam[:],
+                op0=ALU.subtract,
+                op1=ALU.mult,
+            )
+
+        def rsqrt(c):
+            ve = work.tile([P, TILES], F32, name="ve", tag="ve")
+            nc.gpsimd.tensor_scalar(
+                out=ve[:], in0=mv[c][:, :, 1], scalar1=EPS, scalar2=0.0, op0=ALU.add, op1=ALU.add
+            )
+            rstd[c] = work.tile([P, TILES], F32, name="rstd", tag="rstd", bufs=3)
+            nc.gpsimd.tensor_tensor(out=rstd[c][:], in0=ve[:], in1=mhalf[:], op=ALU.pow)
+
+        res = {}
+
+        def norm(c, k):
+            if k == 0:
+                res[c] = work.tile([P, TILES, O], F32, name="res", tag="res", bufs=3)
+            nc.scalar.activation(
+                out=res[c][:, k, :], in_=zs[c][:, k, :], func=ACT.Copy, scale=rstd[c][:, k : k + 1]
+            )
+
+        def store(c):
+            nc.sync.dma_start(out=out_rows[c], in_=res[c][:].rearrange("p r o -> p (r o)"))
+
+        xtp = psum.tile([P, 2, P], F32, name="xtp", tag="yp", bufs=3)
+        for u in range(2):
+            nc.tensor.transpose(xtp[:, u, :], xsb[:].bitcast(F32)[:, u : D // 2 : 2], ident[:])
+        xt = keep.tile([P, 2, P], F32, name="xt", align_bytes=64)
+        nc.vector.tensor_copy(out=xt[:], in_=xtp[:])
+
+        scod, sscl, rcod, rscl = {}, {}, {}, {}
+        sgr, rgr = {}, {}
+
+        def send_copy(q):
+            sgr[q] = work.tile([P, 16 * REP * 4], BF16, name="sgr", tag="sgr", align_bytes=64)
+            nc.scalar.copy(
+                out=sgr[q][:].bitcast(F32).rearrange("p (i r u) -> p i r u", i=16, u=2),
+                in_=xt[:, :, 16 * q : 16 * q + 16]
+                .rearrange("p u i -> p i u")
+                .unsqueeze(2)
+                .to_broadcast([P, 16, REP, 2]),
+            )
+
+        def send_quant(q):
+            scod[q] = work.tile([P, 16 * REP], U32, name="scod", tag="scod", align_bytes=64)
+            sscl[q] = work.tile([P, 16 * REP], U8, name="sscl", tag="sscl", align_bytes=64)
+            nc.vector.quantize_mx(out=scod[q][:].bitcast(FP8X4), scales=sscl[q][:], in_=sgr[q][:])
+
+        def recv_copy(b):
+            rgr[b] = work.tile([P, TILES * P * 4], BF16, name="rgr", tag="rgr", bufs=1, align_bytes=64)
+            for k in range(TILES):
+                nc.scalar.copy(
+                    out=rgr[b][:, k * 512 : (k + 1) * 512]
+                    .bitcast(F32)
+                    .rearrange("p (r j u) -> p r j u", r=SENDERS, u=2),
+                    in_=xt[:, :, b * N + k : (b + 1) * N : TILES]
+                    .rearrange("p u j -> p j u")
+                    .unsqueeze(1)
+                    .to_broadcast([P, SENDERS, N // TILES, 2]),
+                )
+
+        def recv_quant(b):
+            rcod[b] = keep.tile([P, TILES * P], U32, name="rcod%d" % b, align_bytes=64)
+            rscl[b] = keep.tile([P, TILES * P], U8, name="rscl%d" % b, align_bytes=64)
+            nc.vector.quantize_mx(out=rcod[b][:].bitcast(FP8X4), scales=rscl[b][:], in_=rgr[b][:])
+
+        cast(0, 0)
+        cast(0, 1)
+        recv_copy(0)
+        send_copy(0)
+        wper = keep.tile([P, 1536], I32, name="wper", align_bytes=64)
+        sper = keep.tile([P, 1536], U8, name="sper", align_bytes=64)
+
+        def permute(w):
+            cols = slice(w * 512, (w + 1) * 512)
+            nc.vector.tensor_copy(
+                out=wper[:, cols].rearrange("p (t m) -> p t m", t=4),
+                in_=wraw[:, cols].rearrange("p (m t) -> p t m", t=4),
+            )
+            nc.vector.tensor_copy(
+                out=sper[:, cols].rearrange("p (t m) -> p t m", t=4),
+                in_=sraw[:, cols].rearrange("p (m t) -> p t m", t=4),
+            )
+
+        for s in range(CHUNKS + 3):
+            a, m, y, n = s, s - 1, s - 2, s - 3
+            has_a, has_m, has_y, has_n = a < CHUNKS, 0 <= m < CHUNKS, 0 <= y < CHUNKS, 0 <= n < CHUNKS
+            if s >= 1 and s + 2 < CHUNKS:
+                load(s + 2)
+            if has_a:
+                turn(a, 0)
+                apply_scale(a, 0)
+            if s == 0:
+                recv_quant(0)
+                send_quant(0)
+            if has_y:
+                quant_h(y, 1)
+            if has_m:
+                project(m, 0)
+                silu(m, 0)
+                gain(m, 0)
+            if has_y:
+                output(y, 0)
+                bstats(y, 0)
+            if has_n:
+                norm(n, 0)
+            if a + 1 < CHUNKS:
+                cast(a + 1, 0)
+            if has_m:
+                project(m, 1)
+                silu(m, 1)
+                gain(m, 1)
+            if has_y:
+                output(y, 1)
+                bstats(y, 1)
+                baggr(y, 0)
+                center(y, 0)
+            if has_n:
+                norm(n, 1)
+            if has_a:
+                turn(a, 1)
+            if has_y:
+                baggr(y, 1)
+                center(y, 1)
+            if has_a:
+                apply_scale(a, 1)
+            if s == 0:
+                for w in (2, 1, 0):
+                    permute(w)
+            if has_m:
+                quant_h(m, 0)
+                project(m, 2)
+                silu(m, 2)
+                gain(m, 2)
+            if has_y:
+                output(y, 2)
+                bstats(y, 2)
+            if has_n:
+                norm(n, 2)
+            if a + 1 < CHUNKS:
+                cast(a + 1, 1)
+            if has_m:
+                project(m, 3)
+                silu(m, 3)
+                gain(m, 3)
+            if has_y:
+                output(y, 3)
+                bstats(y, 3)
+            if has_a:
+                quant_e(a, 0)
+            if has_y:
+                baggr(y, 2)
+                center(y, 2)
+            if has_n:
+                norm(n, 3)
+            if has_y:
+                baggr(y, 3)
+                center(y, 3)
+            if has_a:
+                quant_e(a, 1)
+            if has_y:
+                rsqrt(y)
+            if has_n:
+                store(n)
+            if s % 2 == 0 and s + 2 < CHUNKS:
+                send_copy(s // 2 + 1)
+                send_quant(s // 2 + 1)
+            if s == CHUNKS_B - 2:
+                recv_copy(1)
+                recv_quant(1)

@@ -24,6 +24,55 @@ SENDERS = CHUNK // N
 REP = P // SENDERS
 EPS = 1e-5
 
+NS = 2
+PROGRAM = (
+    ("Z", 0, 3),
+    ("Ng", 3, 4),
+    ("Z", 1, 3),
+    ("M", 0, 1),
+    ("A", 1, 0),
+    ("A", 0, 0),
+    ("U", 1, 3),
+    ("U", 0, 3),
+    ("N", 0, 4),
+    ("Y", 0, 3),
+    ("M", 1, 1),
+    ("Em", 0, 3),
+    ("Q", 0, 0),
+    ("Y", 2, 3),
+    ("S", 0, 1),
+    ("Y", 3, 3),
+    ("B", 2, 3),
+    ("W", 0, 3),
+    ("S", 1, 1),
+    ("M", 2, 1),
+    ("C", 0, -2),
+    ("N", 2, 4),
+    ("B", 3, 3),
+    ("S", 2, 1),
+    ("H", 0, 2),
+    ("G", 3, 3),
+    ("Y", 1, 3),
+    ("F", 0, 1),
+    ("L", 0, -3),
+    ("G", 2, 3),
+    ("M", 3, 1),
+    ("E", 3, 3),
+    ("T", 1, -1),
+    ("N", 1, 4),
+    ("W", 1, 3),
+    ("O", 0, 4),
+    ("S", 3, 1),
+    ("T", 0, -1),
+    ("E", 2, 3),
+    ("F", 1, 1),
+    ("F", 2, 1),
+    ("C", 1, -3),
+    ("R", 0, 3),
+    ("Em", 1, 3),
+    ("F", 3, 1),
+)
+
 FLOPS = 2 * ROWS * (D * F + F * O) + 2 * B * N * D * 2 * F
 
 
@@ -40,95 +89,73 @@ def tile_meshgraphnetdenseedgeupdate_w8_kernel(
         psum = ctx.enter_context(tc.psum_pool(name="psum", bufs=1))
         ctx.enter_context(tc.manual_schedule())
 
-        ebytes = {}
+        eb, ebf, tr, egr, ecod, escl = {}, {}, {}, {}, {}, {}
+        hp, hsil, hg, hcod, hscl = {}, {}, {}, {}, {}
+        yp, ms, nmu, ssq, st, mv, zs, rstd, res = {}, {}, {}, {}, {}, {}, {}, {}, {}
+        scod, sscl, rcod, rscl, sgr, rgr = {}, {}, {}, {}, {}, {}
 
-        def load(c):
-            t = work.tile([P, TILES * D], U8, name="eb", tag="eb", bufs=4, align_bytes=64)
-            nc.sync.dma_start(out=t[:], in_=e_rows[c])
-            ebytes[c] = t
-
-        load(0)
-        xsb = keep.tile([P, D], BF16, name="xsb", align_bytes=64)
-        nc.sync.dma_start(out=xsb[:], in_=x.rearrange("b i k -> (b i) k"))
-        esc = keep.tile([P, 4], F32, name="esc")
-        nc.sync.dma_start(out=esc[:], in_=e_scale.rearrange("a b c (p t) -> p (a b c t)", t=4))
+        def fresh(where, c, tag, shape, dtype, bufs):
+            if c not in where:
+                where[c] = work.tile(shape, dtype, name=tag, tag=tag, bufs=bufs, align_bytes=64)
+            return where[c]
 
         ident = keep.tile([P, P], F32, name="ident")
         make_identity(nc, ident[:])
         mhalf = keep.tile([P, TILES], F32, name="mhalf")
         nc.gpsimd.memset(mhalf[:], -0.5)
-
+        warm = keep.tile([P, 1], F32, name="warm")
+        nc.vector.memset(warm[:], 0.0)
+        nc.scalar.activation(out=warm[:], in_=warm[:], func=ACT.Silu)
         sraw = keep.tile([P, 2048], U8, name="sraw", align_bytes=64)
         nc.vector.memset(sraw[:].bitcast(I32), 0)
-        for src, lo, n in ((wn_scales, 512, 1024), (we_scales, 0, 512), (w2_scales, 1536, 512)):
-            view = src[0].rearrange("(q r) n -> r q n", r=4)
-            for r in range(4):
-                nc.sync.dma_start(
-                    out=sraw[r:P:32, lo : lo + n].bitcast(I32), in_=view[r].bitcast(I32)
-                )
+        xsb = keep.tile([P, D], BF16, name="xsb", align_bytes=64)
+        esc = keep.tile([P, 4], F32, name="esc")
         wraw = keep.tile([P, 1536], I32, name="wraw", align_bytes=64)
-        nc.sync.dma_start(out=wraw[:, 512:1536], in_=wn_words[0].rearrange("p n t -> p (n t)").bitcast(I32))
-        nc.sync.dma_start(out=wraw[:, 0:512], in_=we_words[0].rearrange("p n t -> p (n t)").bitcast(I32))
         g4 = keep.tile([P, 4], BF16, name="g4")
-        nc.sync.dma_start(out=g4[:], in_=g.rearrange("(p t) -> p t", t=4))
-        load(1)
         w2w = keep.tile([P, O], I32, name="w2w", align_bytes=64)
-        nc.sync.dma_start(out=w2w[:], in_=w2_words[0].rearrange("p n t -> p (n t)").bitcast(I32))
-        load(2)
         gam = keep.tile([P, O], BF16, name="gam")
-        nc.sync.dma_start(out=gam[:], in_=gamma.partition_broadcast(P))
+        xt = keep.tile([P, 2, P], F32, name="xt", align_bytes=64)
+        wper = keep.tile([P, 1536], I32, name="wper", align_bytes=64)
+        sper = keep.tile([P, 1536], U8, name="sper", align_bytes=64)
+        junk = keep.tile([P, O], BF16, name="junk", align_bytes=64)
 
-        ebf = {}
+        def do_L(c, k):
+            t = fresh(eb, c, "eb", [P, TILES * D], U8, 4)
+            nc.sync.dma_start(out=t[:], in_=e_rows[c])
 
-        def cast(c, h):
-            if h == 0:
-                ebf[c] = work.tile([P, TILES * D], BF16, name="ebf", tag="ebf", align_bytes=64)
-            lo = h * 2 * D
-            nc.scalar.copy(out=ebf[c][:, lo : lo + 2 * D], in_=ebytes[c][:, lo : lo + 2 * D].bitcast(FP8))
+        def do_C(c, k):
+            t = fresh(ebf, c, "ebf", [P, TILES * D], BF16, 3)
+            lo = k * 2 * D
+            nc.scalar.copy(out=t[:, lo : lo + 2 * D], in_=eb[c][:, lo : lo + 2 * D].bitcast(FP8))
 
-        trs = {}
-
-        def turn(c, h):
+        def do_T(c, k):
             t = psum.tile([P, 2, 2 * P], F32, name="tr", tag="tr", bufs=2)
             words = ebf[c][:].bitcast(F32)
-            for k in range(2):
-                base = (2 * h + k) * (D // 2)
+            for i in range(2):
+                base = (2 * k + i) * (D // 2)
                 for u in range(2):
                     nc.tensor.transpose(
-                        t[:, u, k * P : (k + 1) * P], words[:, base + u : base + D // 2 : 2], ident[:]
+                        t[:, u, i * P : (i + 1) * P], words[:, base + u : base + D // 2 : 2], ident[:]
                     )
-            trs[c, h] = t
+            tr[c, k] = t
 
-        egr = {}
-
-        def apply_scale(c, h):
-            if h == 0:
-                egr[c] = work.tile([P, CHUNK * 4], BF16, name="egr", tag="egr", align_bytes=64)
-            src = trs[c, h][:].rearrange("p u n -> p (u n)").bitcast(BF16)
+        def do_A(c, k):
+            t = fresh(egr, c, "egr", [P, CHUNK * 4], BF16, 2)
+            src = tr[c, k][:].rearrange("p u n -> p (u n)").bitcast(BF16)
             nc.vector.tensor_tensor(
-                out=egr[c][:, h * 1024 : (h + 1) * 1024].rearrange("p (n u e) -> p n u e", u=2, e=2),
+                out=t[:, k * 1024 : (k + 1) * 1024].rearrange("p (n u e) -> p n u e", u=2, e=2),
                 in0=src.rearrange("p (u n e) -> p n u e", u=2, e=2),
                 in1=esc[:].rearrange("p (u e) -> p u e", e=2).unsqueeze(1).to_broadcast([P, 256, 2, 2]),
                 op=ALU.mult,
             )
 
-        ecod, escl = {}, {}
+        def do_Q(c, k):
+            t = fresh(ecod, c, "ecod", [P, CHUNK], U32, 2)
+            q = fresh(escl, c, "escl", [P, CHUNK], U8, 2)
+            nc.vector.quantize_mx(out=t[:].bitcast(FP8X4), scales=q[:], in_=egr[c][:])
 
-        def quant_e(c, h):
-            if h == 0:
-                ecod[c] = work.tile([P, CHUNK], U32, name="ecod", tag="ecod", align_bytes=64)
-                escl[c] = work.tile([P, CHUNK], U8, name="escl", tag="escl", align_bytes=64)
-            cols = slice(h * 256, (h + 1) * 256)
-            nc.vector.quantize_mx(
-                out=ecod[c][:, cols].bitcast(FP8X4),
-                scales=escl[c][:, cols],
-                in_=egr[c][:, h * 1024 : (h + 1) * 1024],
-            )
-
-        hps, hsil, hg = {}, {}, {}
-
-        def project(c, k):
-            t = psum.tile([P, 4, P], F32, name="hp", tag="hp", bufs=3)
+        def do_M(c, k):
+            t = psum.tile([P, 4, P], F32, name="hp", tag="hp", bufs=2)
             cols = slice(k * P, (k + 1) * P)
             b = c // CHUNKS_B
             scols = slice((c % 2) * P, (c % 2 + 1) * P)
@@ -149,110 +176,123 @@ def tile_meshgraphnetdenseedgeupdate_w8_kernel(
                         start=(i == 0),
                         stop=(i == 2),
                     )
-            hps[c, k] = t
+            hp[c, k] = t
 
-        def silu(c, k):
-            if k == 0:
-                hsil[c] = work.tile([P, CHUNK * 4], F32, name="hsil", tag="hsil", align_bytes=64)
+        def do_S(c, k):
+            t = fresh(hsil, c, "hsil", [P, CHUNK * 4], F32, 2)
             nc.scalar.activation(
-                out=hsil[c][:, k * 512 : (k + 1) * 512].rearrange("p (n t) -> p n t", t=4),
-                in_=hps[c, k][:].rearrange("p t n -> p n t"),
+                out=t[:, k * 512 : (k + 1) * 512].rearrange("p (n t) -> p n t", t=4),
+                in_=hp[c, k][:].rearrange("p t n -> p n t"),
                 func=ACT.Silu,
             )
 
-        def gain(c, k):
-            if k == 0:
-                hg[c] = work.tile([P, CHUNK * 4], BF16, name="hg", tag="hg", align_bytes=64)
+        def do_F(c, k):
+            t = fresh(hg, c, "hg", [P, CHUNK * 4], BF16, 3)
             cols = slice(k * 512, (k + 1) * 512)
-            nc.gpsimd.tensor_tensor(
-                out=hg[c][:, cols].rearrange("p (n t) -> p n t", t=4),
+            eng = nc.gpsimd
+            eng.tensor_tensor(
+                out=t[:, cols].rearrange("p (n t) -> p n t", t=4),
                 in0=hsil[c][:, cols].rearrange("p (n t) -> p n t", t=4),
                 in1=g4[:].unsqueeze(1).to_broadcast([P, P, 4]),
                 op=ALU.mult,
             )
 
-        hcod, hscl = {}, {}
+        def do_H(c, k):
+            t = fresh(hcod, c, "hcod", [P, CHUNK], U32, 3)
+            q = fresh(hscl, c, "hscl", [P, CHUNK], U8, 3)
+            nc.vector.quantize_mx(out=t[:].bitcast(FP8X4), scales=q[:], in_=hg[c][:])
 
-        def quant_h(c, h):
-            if h == 0:
-                hcod[c] = work.tile([P, CHUNK], U32, name="hcod", tag="hcod", align_bytes=64)
-                hscl[c] = work.tile([P, CHUNK], U8, name="hscl", tag="hscl", align_bytes=64)
-            cols = slice(h * 256, (h + 1) * 256)
-            nc.vector.quantize_mx(
-                out=hcod[c][:, cols].bitcast(FP8X4),
-                scales=hscl[c][:, cols],
-                in_=hg[c][:, h * 1024 : (h + 1) * 1024],
-            )
-
-        yps, stats, mv, zs, rstd = {}, {}, {}, {}, {}
-
-        def output(c, k):
-            t = psum.tile([P, O], F32, name="yp", tag="yp", bufs=3)
-            cols = slice(k * P, (k + 1) * P)
+        def out_pass(dst, c, k, cols, start, stop):
+            rows = slice(k * P, (k + 1) * P)
             nc.tensor.matmul_mx(
-                out=t[:],
-                lhsT=hcod[c][:, cols].bitcast(FP8X4),
-                lhsT_scale=hscl[c][:, cols],
-                rhs=w2w[:].bitcast(FP8X4),
-                rhs_scale=sraw[:, 1536:2048],
-                start=True,
-                stop=True,
+                out=dst,
+                lhsT=hcod[c][:, rows].bitcast(FP8X4),
+                lhsT_scale=hscl[c][:, rows],
+                rhs=w2w[:, cols].bitcast(FP8X4),
+                rhs_scale=sraw[:, 1536 + cols.start : 1536 + cols.stop],
+                start=start,
+                stop=stop,
             )
-            yps[c, k] = t
 
-        def bstats(c, k):
-            if k == 0:
-                stats[c] = work.tile([P, TILES, 6], F32, name="stats", tag="stats", bufs=3)
-                mv[c] = work.tile([P, TILES, 2], F32, name="mv", tag="mv", bufs=3)
-                zs[c] = work.tile([P, TILES, O], F32, name="zs", tag="zs")
-            nc.vector.bn_stats(out=stats[c][:, k, :], in_=yps[c, k][:])
+        def do_Y(c, k):
+            yp[c, k] = psum.tile([P, O], F32, name="yp", tag="yp", bufs=3)
+            out_pass(yp[c, k][:], c, k, slice(0, O), True, True)
 
-        def baggr(c, k):
-            nc.vector.bn_aggr(out=mv[c][:, k, :], in_=stats[c][:, k, :])
+        def do_B(c, k):
+            t = fresh(st, c, "st", [P, TILES, 6], F32, 3)
+            nc.vector.bn_stats(out=t[:, k, :], in_=yp[c, k][:])
 
-        def center(c, k):
+        def do_G(c, k):
+            t = fresh(mv, c, "mv", [P, TILES, 2], F32, 3)
+            nc.vector.bn_aggr(out=t[:, k, :], in_=st[c][:, k, :])
+
+        def center(c, k, scalar, op0):
+            t = fresh(zs, c, "zs", [P, TILES, O], F32, 3)
             nc.vector.scalar_tensor_tensor(
-                out=zs[c][:, k, :],
-                in0=yps[c, k][:],
-                scalar=mv[c][:, k, 0:1],
-                in1=gam[:],
-                op0=ALU.subtract,
-                op1=ALU.mult,
+                out=t[:, k, :], in0=yp[c, k][:], scalar=scalar, in1=gam[:], op0=op0, op1=ALU.mult
             )
 
-        def rsqrt(c):
-            ve = work.tile([P, TILES], F32, name="ve", tag="ve")
-            nc.gpsimd.tensor_scalar(
-                out=ve[:], in0=mv[c][:, :, 1], scalar1=EPS, scalar2=0.0, op0=ALU.add, op1=ALU.add
-            )
-            rstd[c] = work.tile([P, TILES], F32, name="rstd", tag="rstd", bufs=3)
-            nc.gpsimd.tensor_tensor(out=rstd[c][:], in0=ve[:], in1=mhalf[:], op=ALU.pow)
+        def do_E(c, k):
+            center(c, k, mv[c][:, k, 0:1], ALU.subtract)
 
-        res = {}
+        def do_Z(c, k):
+            if c not in ms:
+                ms[c] = psum.tile([P, 4, P], F32, name="ms", tag="ms", bufs=1)
+            for i in range(4):
+                out_pass(ms[c][:, k, :], c, k, slice(i * P, (i + 1) * P), i == 0, i == 3)
 
-        def norm(c, k):
-            if k == 0:
-                res[c] = work.tile([P, TILES, O], F32, name="res", tag="res", bufs=3)
+        def do_U(c, k):
+            t = fresh(nmu, c, "nmu", [P, TILES], F32, 3)
             nc.scalar.activation(
-                out=res[c][:, k, :], in_=zs[c][:, k, :], func=ACT.Copy, scale=rstd[c][:, k : k + 1]
+                out=junk[:, 0:P], in_=ms[c][:, k, :], func=ACT.Identity, scale=-1.0 / O, accum_out=t[:, k : k + 1]
             )
 
-        def store(c):
-            nc.sync.dma_start(out=out_rows[c], in_=res[c][:].rearrange("p r o -> p (r o)"))
+        def do_W(c, k):
+            t = fresh(ssq, c, "ssq", [P, TILES], F32, 3)
+            nc.scalar.activation(
+                out=junk[:], in_=yp[c, k][:], func=ACT.Square, bias=nmu[c][:, k : k + 1], accum_out=t[:, k : k + 1]
+            )
 
-        xtp = psum.tile([P, 2, P], F32, name="xtp", tag="yp", bufs=3)
-        for u in range(2):
-            nc.tensor.transpose(xtp[:, u, :], xsb[:].bitcast(F32)[:, u : D // 2 : 2], ident[:])
-        xt = keep.tile([P, 2, P], F32, name="xt", align_bytes=64)
-        nc.vector.tensor_copy(out=xt[:], in_=xtp[:])
+        def do_Em(c, k):
+            center(c, k, nmu[c][:, k : k + 1], ALU.add)
 
-        scod, sscl, rcod, rscl = {}, {}, {}, {}
-        sgr, rgr = {}, {}
+        def do_R(c, k):
+            ve = work.tile([P, TILES], F32, name="ve", tag="ve", bufs=2)
+            if NS > 0:
+                nc.gpsimd.tensor_scalar(
+                    out=ve[:, 0:NS], in0=ssq[c][:, 0:NS], scalar1=1.0 / O, scalar2=EPS, op0=ALU.mult, op1=ALU.add
+                )
+            if NS < TILES:
+                nc.gpsimd.tensor_scalar(
+                    out=ve[:, NS:TILES], in0=mv[c][:, NS:TILES, 1], scalar1=EPS, scalar2=0.0, op0=ALU.add, op1=ALU.add
+                )
+            t = fresh(rstd, c, "rstd", [P, TILES], F32, 3)
+            nc.gpsimd.tensor_tensor(out=t[:], in0=ve[:], in1=mhalf[:], op=ALU.pow)
+
+        def last_store(c, k):
+            if c == CHUNKS - 1:
+                nc.sync.dma_start(out=out_rows[c][:, k * O : (k + 1) * O], in_=res[c][:, k, :])
+
+        def do_N(c, k):
+            t = fresh(res, c, "res", [P, TILES, O], F32, 3)
+            nc.scalar.activation(out=t[:, k, :], in_=zs[c][:, k, :], func=ACT.Copy, scale=rstd[c][:, k : k + 1])
+            last_store(c, k)
+
+        def do_Ng(c, k):
+            t = fresh(res, c, "res", [P, TILES, O], F32, 3)
+            nc.gpsimd.tensor_scalar(
+                out=t[:, k, :], in0=zs[c][:, k, :], scalar1=rstd[c][:, k : k + 1], scalar2=0.0, op0=ALU.mult, op1=ALU.add
+            )
+            last_store(c, k)
+
+        def do_O(c, k):
+            if c < CHUNKS - 1:
+                nc.sync.dma_start(out=out_rows[c], in_=res[c][:].rearrange("p r o -> p (r o)"))
 
         def send_copy(q):
-            sgr[q] = work.tile([P, 16 * REP * 4], BF16, name="sgr", tag="sgr", align_bytes=64)
+            t = fresh(sgr, q, "sgr", [P, 16 * REP * 4], BF16, 2)
             nc.scalar.copy(
-                out=sgr[q][:].bitcast(F32).rearrange("p (i r u) -> p i r u", i=16, u=2),
+                out=t[:].bitcast(F32).rearrange("p (i r u) -> p i r u", i=16, u=2),
                 in_=xt[:, :, 16 * q : 16 * q + 16]
                 .rearrange("p u i -> p i u")
                 .unsqueeze(2)
@@ -260,17 +300,15 @@ def tile_meshgraphnetdenseedgeupdate_w8_kernel(
             )
 
         def send_quant(q):
-            scod[q] = work.tile([P, 16 * REP], U32, name="scod", tag="scod", align_bytes=64)
-            sscl[q] = work.tile([P, 16 * REP], U8, name="sscl", tag="sscl", align_bytes=64)
-            nc.vector.quantize_mx(out=scod[q][:].bitcast(FP8X4), scales=sscl[q][:], in_=sgr[q][:])
+            t = fresh(scod, q, "scod", [P, 16 * REP], U32, 2)
+            v = fresh(sscl, q, "sscl", [P, 16 * REP], U8, 2)
+            nc.vector.quantize_mx(out=t[:].bitcast(FP8X4), scales=v[:], in_=sgr[q][:])
 
         def recv_copy(b):
-            rgr[b] = work.tile([P, TILES * P * 4], BF16, name="rgr", tag="rgr", bufs=1, align_bytes=64)
+            t = fresh(rgr, b, "rgr", [P, TILES * P * 4], BF16, 1)
             for k in range(TILES):
                 nc.scalar.copy(
-                    out=rgr[b][:, k * 512 : (k + 1) * 512]
-                    .bitcast(F32)
-                    .rearrange("p (r j u) -> p r j u", r=SENDERS, u=2),
+                    out=t[:, k * 512 : (k + 1) * 512].bitcast(F32).rearrange("p (r j u) -> p r j u", r=SENDERS, u=2),
                     in_=xt[:, :, b * N + k : (b + 1) * N : TILES]
                     .rearrange("p u j -> p j u")
                     .unsqueeze(1)
@@ -278,111 +316,76 @@ def tile_meshgraphnetdenseedgeupdate_w8_kernel(
                 )
 
         def recv_quant(b):
-            rcod[b] = keep.tile([P, TILES * P], U32, name="rcod%d" % b, align_bytes=64)
-            rscl[b] = keep.tile([P, TILES * P], U8, name="rscl%d" % b, align_bytes=64)
-            nc.vector.quantize_mx(out=rcod[b][:].bitcast(FP8X4), scales=rscl[b][:], in_=rgr[b][:])
-
-        cast(0, 0)
-        cast(0, 1)
-        recv_copy(0)
-        send_copy(0)
-        wper = keep.tile([P, 1536], I32, name="wper", align_bytes=64)
-        sper = keep.tile([P, 1536], U8, name="sper", align_bytes=64)
+            t = fresh(rcod, b, "rcod", [P, TILES * P], U32, 2)
+            v = fresh(rscl, b, "rscl", [P, TILES * P], U8, 2)
+            nc.vector.quantize_mx(out=t[:].bitcast(FP8X4), scales=v[:], in_=rgr[b][:])
 
         def permute(w):
             cols = slice(w * 512, (w + 1) * 512)
-            nc.vector.tensor_copy(
-                out=wper[:, cols].rearrange("p (t m) -> p t m", t=4),
-                in_=wraw[:, cols].rearrange("p (m t) -> p t m", t=4),
-            )
-            nc.vector.tensor_copy(
-                out=sper[:, cols].rearrange("p (t m) -> p t m", t=4),
-                in_=sraw[:, cols].rearrange("p (m t) -> p t m", t=4),
-            )
+            for dst, raw in ((wper, wraw), (sper, sraw)):
+                nc.vector.tensor_copy(
+                    out=dst[:, cols].rearrange("p (t m) -> p t m", t=4),
+                    in_=raw[:, cols].rearrange("p (m t) -> p t m", t=4),
+                )
 
-        for s in range(CHUNKS + 3):
-            a, m, y, n = s, s - 1, s - 2, s - 3
-            has_a, has_m, has_y, has_n = a < CHUNKS, 0 <= m < CHUNKS, 0 <= y < CHUNKS, 0 <= n < CHUNKS
-            if s >= 1 and s + 2 < CHUNKS:
-                load(s + 2)
-            if has_a:
-                turn(a, 0)
-                apply_scale(a, 0)
+        def once(s):
+            if s == -3:
+                nc.sync.dma_start(out=xsb[:], in_=x.rearrange("b i k -> (b i) k"))
+                nc.sync.dma_start(out=esc[:], in_=e_scale.rearrange("a b c (p t) -> p (a b c t)", t=4))
+                for src, lo, n in ((wn_scales, 512, 1024), (we_scales, 0, 512), (w2_scales, 1536, 512)):
+                    view = src[0].rearrange("(q r) n -> r q n", r=4)
+                    for r in range(4):
+                        nc.sync.dma_start(out=sraw[r:P:32, lo : lo + n].bitcast(I32), in_=view[r].bitcast(I32))
+                nc.sync.dma_start(out=wraw[:, 512:1536], in_=wn_words[0].rearrange("p n t -> p (n t)").bitcast(I32))
+                nc.sync.dma_start(out=wraw[:, 0:512], in_=we_words[0].rearrange("p n t -> p (n t)").bitcast(I32))
+                nc.sync.dma_start(out=g4[:], in_=g.rearrange("(p t) -> p t", t=4))
+            if s == -2:
+                nc.sync.dma_start(out=w2w[:], in_=w2_words[0].rearrange("p n t -> p (n t)").bitcast(I32))
+                nc.sync.dma_start(out=gam[:], in_=gamma.partition_broadcast(P))
+            if s == -1:
+                xtp = psum.tile([P, 2, P], F32, name="xtp", tag="yp", bufs=3)
+                for u in range(2):
+                    nc.tensor.transpose(xtp[:, u, :], xsb[:].bitcast(F32)[:, u : D // 2 : 2], ident[:])
+                nc.vector.tensor_copy(out=xt[:], in_=xtp[:])
+                recv_copy(0)
+                send_copy(0)
             if s == 0:
                 recv_quant(0)
                 send_quant(0)
-            if has_y:
-                quant_h(y, 1)
-            if has_m:
-                project(m, 0)
-                silu(m, 0)
-                gain(m, 0)
-            if has_y:
-                output(y, 0)
-                bstats(y, 0)
-            if has_n:
-                norm(n, 0)
-            if a + 1 < CHUNKS:
-                cast(a + 1, 0)
-            if has_m:
-                project(m, 1)
-                silu(m, 1)
-                gain(m, 1)
-            if has_y:
-                output(y, 1)
-                bstats(y, 1)
-                baggr(y, 0)
-                center(y, 0)
-            if has_n:
-                norm(n, 1)
-            if has_a:
-                turn(a, 1)
-            if has_y:
-                baggr(y, 1)
-                center(y, 1)
-            if has_a:
-                apply_scale(a, 1)
-            if s == 0:
                 for w in (2, 1, 0):
                     permute(w)
-            if has_m:
-                quant_h(m, 0)
-                project(m, 2)
-                silu(m, 2)
-                gain(m, 2)
-            if has_y:
-                output(y, 2)
-                bstats(y, 2)
-            if has_n:
-                norm(n, 2)
-            if a + 1 < CHUNKS:
-                cast(a + 1, 1)
-            if has_m:
-                project(m, 3)
-                silu(m, 3)
-                gain(m, 3)
-            if has_y:
-                output(y, 3)
-                bstats(y, 3)
-            if has_a:
-                quant_e(a, 0)
-            if has_y:
-                baggr(y, 2)
-                center(y, 2)
-            if has_n:
-                norm(n, 3)
-            if has_y:
-                baggr(y, 3)
-                center(y, 3)
-            if has_a:
-                quant_e(a, 1)
-            if has_y:
-                rsqrt(y)
-            if has_n:
-                store(n)
-            if s % 2 == 0 and s + 2 < CHUNKS:
+            if s >= 0 and s % 2 == 0 and s + 2 < CHUNKS:
                 send_copy(s // 2 + 1)
                 send_quant(s // 2 + 1)
             if s == CHUNKS_B - 2:
                 recv_copy(1)
                 recv_quant(1)
+
+        steps = {
+            "Z": do_Z,
+            "Ng": do_Ng,
+            "M": do_M,
+            "A": do_A,
+            "U": do_U,
+            "N": do_N,
+            "Y": do_Y,
+            "Em": do_Em,
+            "Q": do_Q,
+            "S": do_S,
+            "B": do_B,
+            "W": do_W,
+            "C": do_C,
+            "H": do_H,
+            "G": do_G,
+            "F": do_F,
+            "L": do_L,
+            "E": do_E,
+            "T": do_T,
+            "O": do_O,
+            "R": do_R,
+        }
+        for s in range(-3, CHUNKS + 4):
+            for op, k, lag in PROGRAM:
+                if 0 <= s - lag < CHUNKS:
+                    steps[op](s - lag, k)
+            once(s)

@@ -24,53 +24,55 @@ SENDERS = CHUNK // N
 REP = P // SENDERS
 EPS = 1e-5
 
-NS = 2
 PROGRAM = (
-    ("Z", 0, 3),
-    ("Ng", 3, 4),
-    ("Z", 1, 3),
-    ("M", 0, 1),
-    ("A", 1, 0),
-    ("A", 0, 0),
-    ("U", 1, 3),
-    ("U", 0, 3),
-    ("N", 0, 4),
-    ("Y", 0, 3),
-    ("M", 1, 1),
-    ("Em", 0, 3),
-    ("Q", 0, 0),
-    ("Y", 2, 3),
-    ("S", 0, 1),
-    ("Y", 3, 3),
-    ("B", 2, 3),
-    ("W", 0, 3),
-    ("S", 1, 1),
-    ("M", 2, 1),
-    ("C", 0, -2),
-    ("N", 2, 4),
-    ("B", 3, 3),
-    ("S", 2, 1),
-    ("H", 0, 2),
-    ("G", 3, 3),
-    ("Y", 1, 3),
-    ("F", 0, 1),
-    ("L", 0, -3),
-    ("G", 2, 3),
-    ("M", 3, 1),
-    ("E", 3, 3),
-    ("T", 1, -1),
-    ("N", 1, 4),
-    ("W", 1, 3),
-    ("O", 0, 4),
-    ("S", 3, 1),
-    ("T", 0, -1),
-    ("E", 2, 3),
-    ("F", 1, 1),
-    ("F", 2, 1),
-    ("C", 1, -3),
-    ("R", 0, 3),
-    ("Em", 1, 3),
-    ("F", 3, 1),
+    ("Z", 6, 3, (1,)),
+    ("U", 6, 3, (1,)),
+    ("C", 0, -3, (0, 1)),
+    ("Y", 2, 3, (0, 1)),
+    ("Z", 5, 3, (0, 1)),
+    ("Y", 0, 3, (0, 1)),
+    ("U", 5, 3, (0, 1)),
+    ("M", 0, 1, (0, 1)),
+    ("B", 2, 3, (0, 1)),
+    ("A", 0, 0, (0, 1)),
+    ("G", 2, 3, (0, 1)),
+    ("Em", 0, 3, (0, 1)),
+    ("Ng", 3, 4, (0, 1)),
+    ("E", 2, 3, (0, 1)),
+    ("N", 2, 4, (0, 1)),
+    ("Y", 1, 3, (0, 1)),
+    ("N", 0, 4, (0, 1)),
+    ("M", 1, 1, (0, 1)),
+    ("B", 1, 3, (0,)),
+    ("S", 0, 1, (0, 1)),
+    ("S", 1, 1, (0, 1)),
+    ("M", 2, 1, (0, 1)),
+    ("L", 0, -5, (0, 1)),
+    ("A", 1, 0, (0, 1)),
+    ("Y", 3, 3, (0, 1)),
+    ("G", 1, 3, (0,)),
+    ("B", 3, 3, (0, 1)),
+    ("W", 1, 3, (1,)),
+    ("W", 0, 3, (0, 1)),
+    ("C", 1, -3, (0, 1)),
+    ("J", 1, 3, (1,)),
+    ("J", 0, 3, (0, 1)),
+    ("H", 0, 2, (0, 1)),
+    ("G", 3, 3, (0, 1)),
+    ("N", 1, 4, (0, 1)),
+    ("E", 1, 3, (0,)),
+    ("O", 0, 4, (0, 1)),
+    ("Q", 0, 0, (0, 1)),
+    ("M", 3, 1, (0, 1)),
+    ("T", 0, -1, (0, 1)),
+    ("F", 0, 1, (0, 1)),
+    ("R", 0, 3, (0, 1)),
+    ("T", 1, -1, (0, 1)),
+    ("S", 3, 1, (0, 1)),
+    ("S", 2, 1, (0, 1)),
+    ("E", 3, 3, (0, 1)),
+    ("F", 1, 1, (0, 1)),
+    ("Em", 1, 3, (1,)),
 )
 
 FLOPS = 2 * ROWS * (D * F + F * O) + 2 * B * N * D * 2 * F
@@ -101,6 +103,15 @@ def tile_meshgraphnetdenseedgeupdate_w8_kernel(
 
         ident = keep.tile([P, P], F32, name="ident")
         make_identity(nc, ident[:])
+        gbig = keep.tile([P, 1024], BF16, name="gbig", align_bytes=64)
+        stk = []
+        for i in range(3):
+            t = keep.tile([P, TILES, 9], F32, name="st%d" % i)
+            nc.gpsimd.memset(t[:], 0.0)
+            nc.gpsimd.tensor_scalar(
+                out=t[:, :, 8], in0=t[:, :, 7], scalar1=1.0, scalar2=O * EPS, op0=ALU.mult, op1=ALU.add
+            )
+            stk.append(t)
         mhalf = keep.tile([P, TILES], F32, name="mhalf")
         nc.gpsimd.memset(mhalf[:], -0.5)
         warm = keep.tile([P, 1], F32, name="warm")
@@ -120,7 +131,7 @@ def tile_meshgraphnetdenseedgeupdate_w8_kernel(
         junk = keep.tile([P, O], BF16, name="junk", align_bytes=64)
 
         def do_L(c, k):
-            t = fresh(eb, c, "eb", [P, TILES * D], U8, 4)
+            t = fresh(eb, c, "eb", [P, TILES * D], U8, 6)
             nc.sync.dma_start(out=t[:], in_=e_rows[c])
 
         def do_C(c, k):
@@ -155,7 +166,7 @@ def tile_meshgraphnetdenseedgeupdate_w8_kernel(
             nc.vector.quantize_mx(out=t[:].bitcast(FP8X4), scales=q[:], in_=egr[c][:])
 
         def do_M(c, k):
-            t = psum.tile([P, 4, P], F32, name="hp", tag="hp", bufs=2)
+            t = psum.tile([P, 4, P], F32, name="hp", tag="hp", bufs=3)
             cols = slice(k * P, (k + 1) * P)
             b = c // CHUNKS_B
             scols = slice((c % 2) * P, (c % 2 + 1) * P)
@@ -188,14 +199,9 @@ def tile_meshgraphnetdenseedgeupdate_w8_kernel(
 
         def do_F(c, k):
             t = fresh(hg, c, "hg", [P, CHUNK * 4], BF16, 3)
-            cols = slice(k * 512, (k + 1) * 512)
-            eng = nc.gpsimd
-            eng.tensor_tensor(
-                out=t[:, cols].rearrange("p (n t) -> p n t", t=4),
-                in0=hsil[c][:, cols].rearrange("p (n t) -> p n t", t=4),
-                in1=g4[:].unsqueeze(1).to_broadcast([P, P, 4]),
-                op=ALU.mult,
-            )
+            cols = slice(k * 1024, (k + 1) * 1024)
+            eng = nc.vector if (c, k) in ((0, 0),) else nc.gpsimd
+            eng.tensor_tensor(out=t[:, cols], in0=hsil[c][:, cols], in1=gbig[:], op=ALU.mult)
 
         def do_H(c, k):
             t = fresh(hcod, c, "hcod", [P, CHUNK], U32, 3)
@@ -219,12 +225,11 @@ def tile_meshgraphnetdenseedgeupdate_w8_kernel(
             out_pass(yp[c, k][:], c, k, slice(0, O), True, True)
 
         def do_B(c, k):
-            t = fresh(st, c, "st", [P, TILES, 6], F32, 3)
-            nc.vector.bn_stats(out=t[:, k, :], in_=yp[c, k][:])
+            nc.vector.bn_stats(out=stk[c % 3][:, k, 0:6], in_=yp[c, k][:])
 
         def do_G(c, k):
             t = fresh(mv, c, "mv", [P, TILES, 2], F32, 3)
-            nc.vector.bn_aggr(out=t[:, k, :], in_=st[c][:, k, :])
+            nc.vector.bn_aggr(out=t[:, k, :], in_=stk[c % 3][:, k, :])
 
         def center(c, k, scalar, op0):
             t = fresh(zs, c, "zs", [P, TILES, O], F32, 3)
@@ -236,38 +241,35 @@ def tile_meshgraphnetdenseedgeupdate_w8_kernel(
             center(c, k, mv[c][:, k, 0:1], ALU.subtract)
 
         def do_Z(c, k):
-            if c not in ms:
-                ms[c] = psum.tile([P, 4, P], F32, name="ms", tag="ms", bufs=1)
+            t = psum.tile([P, 4, P], F32, name="hp", tag="hp", bufs=3)
             for i in range(4):
-                out_pass(ms[c][:, k, :], c, k, slice(i * P, (i + 1) * P), i == 0, i == 3)
+                out_pass(t[:, 0, :], c, k - 5, slice(i * P, (i + 1) * P), i == 0, i == 3)
+            ms[c, k - 5] = t
 
         def do_U(c, k):
             t = fresh(nmu, c, "nmu", [P, TILES], F32, 3)
+            j = work.tile([P, P], BF16, name="ju", tag="ju", bufs=2)
             nc.scalar.activation(
-                out=junk[:, 0:P], in_=ms[c][:, k, :], func=ACT.Identity, scale=-1.0 / O, accum_out=t[:, k : k + 1]
+                out=j[:], in_=ms[c, k - 5][:, 0, :], func=ACT.Identity, scale=-1.0 / O, accum_out=t[:, k - 5 : k - 4]
             )
 
         def do_W(c, k):
             t = fresh(ssq, c, "ssq", [P, TILES], F32, 3)
+            j = work.tile([P, O], BF16, name="jw", tag="jw", bufs=2)
             nc.scalar.activation(
-                out=junk[:], in_=yp[c, k][:], func=ACT.Square, bias=nmu[c][:, k : k + 1], accum_out=t[:, k : k + 1]
+                out=j[:], in_=yp[c, k][:], func=ACT.Square, bias=nmu[c][:, k : k + 1], accum_out=t[:, k : k + 1]
             )
+
+        def do_J(c, k):
+            t = fresh(mv, c, "mv", [P, TILES, 2], F32, 3)
+            nc.scalar.activation(out=t[:, k, 1:2], in_=ssq[c][:, k : k + 1], func=ACT.Copy, scale=1.0 / O, bias=EPS)
 
         def do_Em(c, k):
             center(c, k, nmu[c][:, k : k + 1], ALU.add)
 
         def do_R(c, k):
-            ve = work.tile([P, TILES], F32, name="ve", tag="ve", bufs=2)
-            if NS > 0:
-                nc.gpsimd.tensor_scalar(
-                    out=ve[:, 0:NS], in0=ssq[c][:, 0:NS], scalar1=1.0 / O, scalar2=EPS, op0=ALU.mult, op1=ALU.add
-                )
-            if NS < TILES:
-                nc.gpsimd.tensor_scalar(
-                    out=ve[:, NS:TILES], in0=mv[c][:, NS:TILES, 1], scalar1=EPS, scalar2=0.0, op0=ALU.add, op1=ALU.add
-                )
             t = fresh(rstd, c, "rstd", [P, TILES], F32, 3)
-            nc.gpsimd.tensor_tensor(out=t[:], in0=ve[:], in1=mhalf[:], op=ALU.pow)
+            nc.gpsimd.tensor_tensor(out=t[:], in0=mv[c][:, :, 1], in1=mhalf[:], op=ALU.pow)
 
         def last_store(c, k):
             if c == CHUNKS - 1:
@@ -275,7 +277,12 @@ def tile_meshgraphnetdenseedgeupdate_w8_kernel(
 
         def do_N(c, k):
             t = fresh(res, c, "res", [P, TILES, O], F32, 3)
-            nc.scalar.activation(out=t[:, k, :], in_=zs[c][:, k, :], func=ACT.Copy, scale=rstd[c][:, k : k + 1])
+            if c == CHUNKS - 1 and k == 2:
+                nc.vector.tensor_scalar(
+                    out=t[:, k, :], in0=zs[c][:, k, :], scalar1=rstd[c][:, k : k + 1], scalar2=None, op0=ALU.mult
+                )
+            else:
+                nc.scalar.activation(out=t[:, k, :], in_=zs[c][:, k, :], func=ACT.Copy, scale=rstd[c][:, k : k + 1])
             last_store(c, k)
 
         def do_Ng(c, k):
@@ -291,9 +298,11 @@ def tile_meshgraphnetdenseedgeupdate_w8_kernel(
 
         def send_copy(q):
             t = fresh(sgr, q, "sgr", [P, 16 * REP * 4], BF16, 2)
-            nc.scalar.copy(
-                out=t[:].bitcast(F32).rearrange("p (i r u) -> p i r u", i=16, u=2),
-                in_=xt[:, :, 16 * q : 16 * q + 16]
+            eng = nc.vector if q == 0 else nc.gpsimd
+            eng.tensor_copy(
+                out=t[:].bitcast(I32).rearrange("p (i r u) -> p i r u", i=16, u=2),
+                in_=xt[:].rearrange("p u n -> p (u n)").bitcast(I32)
+                .rearrange("p (u n) -> p u n", u=2)[:, :, 16 * q : 16 * q + 16]
                 .rearrange("p u i -> p i u")
                 .unsqueeze(2)
                 .to_broadcast([P, 16, REP, 2]),
@@ -320,72 +329,79 @@ def tile_meshgraphnetdenseedgeupdate_w8_kernel(
             v = fresh(rscl, b, "rscl", [P, TILES * P], U8, 2)
             nc.vector.quantize_mx(out=t[:].bitcast(FP8X4), scales=v[:], in_=rgr[b][:])
 
-        def permute(w):
-            cols = slice(w * 512, (w + 1) * 512)
+        def permute():
             for dst, raw in ((wper, wraw), (sper, sraw)):
                 nc.vector.tensor_copy(
-                    out=dst[:, cols].rearrange("p (t m) -> p t m", t=4),
-                    in_=raw[:, cols].rearrange("p (m t) -> p t m", t=4),
+                    out=dst[:].rearrange("p (w t m) -> p w t m", w=3, t=4),
+                    in_=raw[:, 0:1536].rearrange("p (w m t) -> p w t m", w=3, t=4),
                 )
 
+        def scale_rows(src, lo, n):
+            view = src[0].rearrange("(q r) n -> r q n", r=4)
+            for r in range(4):
+                nc.sync.dma_start(out=sraw[r:P:32, lo : lo + n].bitcast(I32), in_=view[r].bitcast(I32))
+
         def once(s):
-            if s == -3:
+            if s == -5:
                 nc.sync.dma_start(out=xsb[:], in_=x.rearrange("b i k -> (b i) k"))
                 nc.sync.dma_start(out=esc[:], in_=e_scale.rearrange("a b c (p t) -> p (a b c t)", t=4))
-                for src, lo, n in ((wn_scales, 512, 1024), (we_scales, 0, 512), (w2_scales, 1536, 512)):
-                    view = src[0].rearrange("(q r) n -> r q n", r=4)
-                    for r in range(4):
-                        nc.sync.dma_start(out=sraw[r:P:32, lo : lo + n].bitcast(I32), in_=view[r].bitcast(I32))
+                scale_rows(wn_scales, 512, 1024)
                 nc.sync.dma_start(out=wraw[:, 512:1536], in_=wn_words[0].rearrange("p n t -> p (n t)").bitcast(I32))
+                scale_rows(we_scales, 0, 512)
                 nc.sync.dma_start(out=wraw[:, 0:512], in_=we_words[0].rearrange("p n t -> p (n t)").bitcast(I32))
                 nc.sync.dma_start(out=g4[:], in_=g.rearrange("(p t) -> p t", t=4))
-            if s == -2:
-                nc.sync.dma_start(out=w2w[:], in_=w2_words[0].rearrange("p n t -> p (n t)").bitcast(I32))
-                nc.sync.dma_start(out=gam[:], in_=gamma.partition_broadcast(P))
-            if s == -1:
                 xtp = psum.tile([P, 2, P], F32, name="xtp", tag="yp", bufs=3)
                 for u in range(2):
                     nc.tensor.transpose(xtp[:, u, :], xsb[:].bitcast(F32)[:, u : D // 2 : 2], ident[:])
                 nc.vector.tensor_copy(out=xt[:], in_=xtp[:])
-                recv_copy(0)
                 send_copy(0)
-            if s == 0:
-                recv_quant(0)
                 send_quant(0)
-                for w in (2, 1, 0):
-                    permute(w)
+                permute()
+                nc.gpsimd.tensor_copy(
+                    out=gbig[:].rearrange("p (n t) -> p n t", t=4), in_=g4[:].unsqueeze(1).to_broadcast([P, 256, 4])
+                )
+            if s == -4:
+                scale_rows(w2_scales, 1536, 512)
+                nc.sync.dma_start(out=w2w[:], in_=w2_words[0].rearrange("p n t -> p (n t)").bitcast(I32))
+                nc.sync.dma_start(out=gam[:], in_=gamma.partition_broadcast(P))
+            if s == -1:
+                recv_copy(0)
+                recv_quant(0)
             if s >= 0 and s % 2 == 0 and s + 2 < CHUNKS:
                 send_copy(s // 2 + 1)
-                send_quant(s // 2 + 1)
-            if s == CHUNKS_B - 2:
+            if s >= 0 and s % 2 == 1 and s + 1 < CHUNKS:
+                send_quant((s + 1) // 2)
+            if s == CHUNKS_B - 3:
                 recv_copy(1)
+            if s == CHUNKS_B - 2:
                 recv_quant(1)
 
         steps = {
             "Z": do_Z,
-            "Ng": do_Ng,
-            "M": do_M,
-            "A": do_A,
             "U": do_U,
-            "N": do_N,
-            "Y": do_Y,
-            "Em": do_Em,
-            "Q": do_Q,
-            "S": do_S,
-            "B": do_B,
-            "W": do_W,
             "C": do_C,
-            "H": do_H,
+            "Y": do_Y,
+            "M": do_M,
+            "B": do_B,
+            "A": do_A,
             "G": do_G,
-            "F": do_F,
-            "L": do_L,
+            "Em": do_Em,
+            "Ng": do_Ng,
             "E": do_E,
-            "T": do_T,
+            "N": do_N,
+            "S": do_S,
+            "L": do_L,
+            "W": do_W,
+            "J": do_J,
+            "H": do_H,
             "O": do_O,
+            "Q": do_Q,
+            "T": do_T,
+            "F": do_F,
             "R": do_R,
         }
-        for s in range(-3, CHUNKS + 4):
-            for op, k, lag in PROGRAM:
-                if 0 <= s - lag < CHUNKS:
+        for s in range(-5, CHUNKS + 4):
+            for op, k, lag, par in PROGRAM:
+                if 0 <= s - lag < CHUNKS and (s - lag) % 2 in par:
                     steps[op](s - lag, k)
             once(s)

@@ -25,54 +25,49 @@ REP = P // SENDERS
 EPS = 1e-5
 
 PROGRAM = (
-    ("Z", 6, 3, (1,)),
-    ("U", 6, 3, (1,)),
-    ("C", 0, -3, (0, 1)),
+    ("C", 1, -3, (0, 1)),
+    ("A", 1, 0, (0, 1)),
     ("Y", 2, 3, (0, 1)),
     ("Z", 5, 3, (0, 1)),
     ("Y", 0, 3, (0, 1)),
-    ("U", 5, 3, (0, 1)),
-    ("M", 0, 1, (0, 1)),
     ("B", 2, 3, (0, 1)),
-    ("A", 0, 0, (0, 1)),
+    ("Y", 1, 3, (0, 1)),
+    ("B", 1, 3, (0, 1)),
+    ("M", 0, 1, (0, 1)),
+    ("U", 5, 3, (0, 1)),
     ("G", 2, 3, (0, 1)),
     ("Em", 0, 3, (0, 1)),
-    ("Ng", 3, 4, (0, 1)),
     ("E", 2, 3, (0, 1)),
-    ("N", 2, 4, (0, 1)),
-    ("Y", 1, 3, (0, 1)),
-    ("N", 0, 4, (0, 1)),
     ("M", 1, 1, (0, 1)),
-    ("B", 1, 3, (0,)),
+    ("N", 2, 4, (0, 1)),
+    ("N", 0, 4, (0, 1)),
     ("S", 0, 1, (0, 1)),
-    ("S", 1, 1, (0, 1)),
+    ("A", 0, 0, (0, 1)),
     ("M", 2, 1, (0, 1)),
     ("L", 0, -5, (0, 1)),
-    ("A", 1, 0, (0, 1)),
+    ("G", 1, 3, (0, 1)),
+    ("S", 1, 1, (0, 1)),
     ("Y", 3, 3, (0, 1)),
-    ("G", 1, 3, (0,)),
-    ("B", 3, 3, (0, 1)),
-    ("W", 1, 3, (1,)),
-    ("W", 0, 3, (0, 1)),
-    ("C", 1, -3, (0, 1)),
-    ("J", 1, 3, (1,)),
-    ("J", 0, 3, (0, 1)),
-    ("H", 0, 2, (0, 1)),
-    ("G", 3, 3, (0, 1)),
     ("N", 1, 4, (0, 1)),
-    ("E", 1, 3, (0,)),
-    ("O", 0, 4, (0, 1)),
+    ("B", 3, 3, (0, 1)),
+    ("H", 0, 2, (0, 1)),
     ("Q", 0, 0, (0, 1)),
+    ("W", 0, 3, (0, 1)),
     ("M", 3, 1, (0, 1)),
-    ("T", 0, -1, (0, 1)),
-    ("F", 0, 1, (0, 1)),
-    ("R", 0, 3, (0, 1)),
-    ("T", 1, -1, (0, 1)),
-    ("S", 3, 1, (0, 1)),
     ("S", 2, 1, (0, 1)),
+    ("G", 3, 3, (0, 1)),
+    ("J", 0, 3, (0, 1)),
+    ("F", 0, 1, (0, 1)),
+    ("E", 1, 3, (0, 1)),
+    ("T", 1, -1, (0, 1)),
     ("E", 3, 3, (0, 1)),
+    ("R", 0, 3, (0, 1)),
+    ("C", 0, -2, (0, 1)),
+    ("N", 3, 4, (0, 1)),
+    ("T", 0, -1, (0, 1)),
+    ("O", 0, 4, (0, 1)),
+    ("S", 3, 1, (0, 1)),
     ("F", 1, 1, (0, 1)),
-    ("Em", 1, 3, (1,)),
 )
 
 FLOPS = 2 * ROWS * (D * F + F * O) + 2 * B * N * D * 2 * F
@@ -166,34 +161,36 @@ def tile_meshgraphnetdenseedgeupdate_w8_kernel(
             nc.vector.quantize_mx(out=t[:].bitcast(FP8X4), scales=q[:], in_=egr[c][:])
 
         def do_M(c, k):
-            t = psum.tile([P, 4, P], F32, name="hp", tag="hp", bufs=3)
-            cols = slice(k * P, (k + 1) * P)
+            t = psum.tile([P, 2, 2 * P], F32, name="hp", tag="hp", bufs=3)
+            cols = slice(k // 2 * 256, (k // 2 + 1) * 256)
             b = c // CHUNKS_B
             scols = slice((c % 2) * P, (c % 2 + 1) * P)
-            moving = (
-                (rcod[b][:, cols], rscl[b][:, cols], 1024),
-                (scod[c // 2][:, scols], sscl[c // 2][:, scols], 512),
-                (ecod[c][:, cols], escl[c][:, cols], 0),
-            )
-            for j in range(4):
-                for i, (codes, scales, w0) in enumerate(moving):
-                    w = slice(w0 + j * P, w0 + (j + 1) * P)
-                    nc.tensor.matmul_mx(
-                        out=t[:, j, :],
-                        lhsT=wper[:, w].bitcast(FP8X4),
-                        lhsT_scale=sper[:, w],
-                        rhs=codes.bitcast(FP8X4),
-                        rhs_scale=scales,
-                        start=(i == 0),
-                        stop=(i == 2),
-                    )
+
+            def add(dst, codes, scales, w0, j, start, stop):
+                w = slice(w0 + j * P, w0 + (j + 1) * P)
+                nc.tensor.matmul_mx(
+                    out=dst,
+                    lhsT=wper[:, w].bitcast(FP8X4),
+                    lhsT_scale=sper[:, w],
+                    rhs=codes.bitcast(FP8X4),
+                    rhs_scale=scales,
+                    start=start,
+                    stop=stop,
+                )
+
+            for e in range(2):
+                j = 2 * (k % 2) + e
+                add(t[:, e, :], rcod[b][:, cols], rscl[b][:, cols], 1024, j, True, False)
+                for i in range(2):
+                    add(t[:, e, i * P : (i + 1) * P], scod[c // 2][:, scols], sscl[c // 2][:, scols], 512, j, False, False)
+                add(t[:, e, :], ecod[c][:, cols], escl[c][:, cols], 0, j, False, True)
             hp[c, k] = t
 
         def do_S(c, k):
             t = fresh(hsil, c, "hsil", [P, CHUNK * 4], F32, 2)
             nc.scalar.activation(
-                out=t[:, k * 512 : (k + 1) * 512].rearrange("p (n t) -> p n t", t=4),
-                in_=hp[c, k][:].rearrange("p t n -> p n t"),
+                out=t[:, k * 512 : (k + 1) * 512].rearrange("p (n e) -> p n e", e=2),
+                in_=hp[c, k][:].rearrange("p e n -> p n e"),
                 func=ACT.Silu,
             )
 
@@ -201,7 +198,12 @@ def tile_meshgraphnetdenseedgeupdate_w8_kernel(
             t = fresh(hg, c, "hg", [P, CHUNK * 4], BF16, 3)
             cols = slice(k * 1024, (k + 1) * 1024)
             eng = nc.vector if (c, k) in ((0, 0),) else nc.gpsimd
-            eng.tensor_tensor(out=t[:, cols], in0=hsil[c][:, cols], in1=gbig[:], op=ALU.mult)
+            eng.tensor_tensor(
+                out=t[:, cols].rearrange("p (n q e) -> p n q e", q=2, e=2),
+                in0=hsil[c][:, cols].rearrange("p (q n e) -> p n q e", q=2, e=2),
+                in1=gbig[:].rearrange("p (n q e) -> p n q e", q=2, e=2),
+                op=ALU.mult,
+            )
 
         def do_H(c, k):
             t = fresh(hcod, c, "hcod", [P, CHUNK], U32, 3)
@@ -241,16 +243,16 @@ def tile_meshgraphnetdenseedgeupdate_w8_kernel(
             center(c, k, mv[c][:, k, 0:1], ALU.subtract)
 
         def do_Z(c, k):
-            t = psum.tile([P, 4, P], F32, name="hp", tag="hp", bufs=3)
+            t = psum.tile([P, 2, 2 * P], F32, name="hp", tag="hp", bufs=3)
             for i in range(4):
-                out_pass(t[:, 0, :], c, k - 5, slice(i * P, (i + 1) * P), i == 0, i == 3)
+                out_pass(t[:, 0, 0:P], c, k - 5, slice(i * P, (i + 1) * P), i == 0, i == 3)
             ms[c, k - 5] = t
 
         def do_U(c, k):
             t = fresh(nmu, c, "nmu", [P, TILES], F32, 3)
             j = work.tile([P, P], BF16, name="ju", tag="ju", bufs=2)
             nc.scalar.activation(
-                out=j[:], in_=ms[c, k - 5][:, 0, :], func=ACT.Identity, scale=-1.0 / O, accum_out=t[:, k - 5 : k - 4]
+                out=j[:], in_=ms[c, k - 5][:, 0, 0:P], func=ACT.Identity, scale=-1.0 / O, accum_out=t[:, k - 5 : k - 4]
             )
 
         def do_W(c, k):
@@ -377,28 +379,27 @@ def tile_meshgraphnetdenseedgeupdate_w8_kernel(
                 recv_quant(1)
 
         steps = {
-            "Z": do_Z,
-            "U": do_U,
             "C": do_C,
-            "Y": do_Y,
-            "M": do_M,
-            "B": do_B,
             "A": do_A,
+            "Y": do_Y,
+            "Z": do_Z,
+            "B": do_B,
+            "M": do_M,
+            "U": do_U,
             "G": do_G,
             "Em": do_Em,
-            "Ng": do_Ng,
             "E": do_E,
             "N": do_N,
             "S": do_S,
             "L": do_L,
+            "H": do_H,
+            "Q": do_Q,
             "W": do_W,
             "J": do_J,
-            "H": do_H,
-            "O": do_O,
-            "Q": do_Q,
-            "T": do_T,
             "F": do_F,
+            "T": do_T,
             "R": do_R,
+            "O": do_O,
         }
         for s in range(-5, CHUNKS + 4):
             for op, k, lag, par in PROGRAM:

from contextlib import ExitStack

import concourse.mybir as mybir
from concourse.masks import make_identity

F32 = mybir.dt.float32
BF16 = mybir.dt.bfloat16
I32 = mybir.dt.int32
U32 = mybir.dt.uint32
U8 = mybir.dt.uint8
FP8 = mybir.dt.float8_e4m3fn
FP8X4 = mybir.dt.float8_e4m3fn_x4
ACT = mybir.ActivationFunctionType
ALU = mybir.AluOpType

P = 128
B, N, D, F, O = 2, 64, 512, 512, 512
ROWS = B * N * N
CHUNK = 512
TILES = CHUNK // P
CHUNKS = ROWS // CHUNK
CHUNKS_B = CHUNKS // B
SENDERS = CHUNK // N
REP = P // SENDERS
EPS = 1e-5

PROGRAM = (
    ("C", 1, -3, (0, 1)),
    ("A", 1, 0, (0, 1)),
    ("Y", 2, 3, (0, 1)),
    ("Z", 5, 3, (0, 1)),
    ("Y", 0, 3, (0, 1)),
    ("B", 2, 3, (0, 1)),
    ("Y", 1, 3, (0, 1)),
    ("B", 1, 3, (0, 1)),
    ("M", 0, 1, (0, 1)),
    ("U", 5, 3, (0, 1)),
    ("G", 2, 3, (0, 1)),
    ("Em", 0, 3, (0, 1)),
    ("E", 2, 3, (0, 1)),
    ("M", 1, 1, (0, 1)),
    ("N", 2, 4, (0, 1)),
    ("N", 0, 4, (0, 1)),
    ("S", 0, 1, (0, 1)),
    ("A", 0, 0, (0, 1)),
    ("M", 2, 1, (0, 1)),
    ("L", 0, -5, (0, 1)),
    ("G", 1, 3, (0, 1)),
    ("S", 1, 1, (0, 1)),
    ("Y", 3, 3, (0, 1)),
    ("N", 1, 4, (0, 1)),
    ("B", 3, 3, (0, 1)),
    ("H", 0, 2, (0, 1)),
    ("Q", 0, 0, (0, 1)),
    ("W", 0, 3, (0, 1)),
    ("M", 3, 1, (0, 1)),
    ("S", 2, 1, (0, 1)),
    ("G", 3, 3, (0, 1)),
    ("J", 0, 3, (0, 1)),
    ("F", 0, 1, (0, 1)),
    ("E", 1, 3, (0, 1)),
    ("T", 1, -1, (0, 1)),
    ("E", 3, 3, (0, 1)),
    ("R", 0, 3, (0, 1)),
    ("C", 0, -2, (0, 1)),
    ("N", 3, 4, (0, 1)),
    ("T", 0, -1, (0, 1)),
    ("O", 0, 4, (0, 1)),
    ("S", 3, 1, (0, 1)),
    ("F", 1, 1, (0, 1)),
)

FLOPS = 2 * ROWS * (D * F + F * O) + 2 * B * N * D * 2 * F


def tile_meshgraphnetdenseedgeupdate_w8_kernel(
    tc, e_bytes, e_scale, x, we_words, we_scales, wn_words, wn_scales, g, w2_words, w2_scales, gamma, out
):
    nc = tc.nc
    e_rows = e_bytes.rearrange("b i j k -> (b i j) k").rearrange("(c p r) k -> c p (r k)", p=P, r=TILES)
    out_rows = out.rearrange("b i j o -> (b i j) o").rearrange("(c p r) o -> c p (r o)", p=P, r=TILES)

    with ExitStack() as ctx:
        keep = ctx.enter_context(tc.tile_pool(name="keep", bufs=1))
        work = ctx.enter_context(tc.tile_pool(name="work", bufs=2))
        psum = ctx.enter_context(tc.psum_pool(name="psum", bufs=1))
        ctx.enter_context(tc.manual_schedule())

        eb, ebf, tr, egr, ecod, escl = {}, {}, {}, {}, {}, {}
        hp, hsil, hg, hcod, hscl = {}, {}, {}, {}, {}
        yp, ms, nmu, ssq, st, mv, zs, rstd, res = {}, {}, {}, {}, {}, {}, {}, {}, {}
        scod, sscl, rcod, rscl, sgr, rgr = {}, {}, {}, {}, {}, {}

        def fresh(where, c, tag, shape, dtype, bufs):
            if c not in where:
                where[c] = work.tile(shape, dtype, name=tag, tag=tag, bufs=bufs, align_bytes=64)
            return where[c]

        ident = keep.tile([P, P], F32, name="ident")
        make_identity(nc, ident[:])
        gbig = keep.tile([P, 1024], BF16, name="gbig", align_bytes=64)
        stk = []
        for i in range(3):
            t = keep.tile([P, TILES, 9], F32, name="st%d" % i)
            nc.gpsimd.memset(t[:], 0.0)
            nc.gpsimd.tensor_scalar(
                out=t[:, :, 8], in0=t[:, :, 7], scalar1=1.0, scalar2=O * EPS, op0=ALU.mult, op1=ALU.add
            )
            stk.append(t)
        mhalf = keep.tile([P, TILES], F32, name="mhalf")
        nc.gpsimd.memset(mhalf[:], -0.5)
        warm = keep.tile([P, 1], F32, name="warm")
        nc.vector.memset(warm[:], 0.0)
        nc.scalar.activation(out=warm[:], in_=warm[:], func=ACT.Silu)
        sraw = keep.tile([P, 2048], U8, name="sraw", align_bytes=64)
        nc.vector.memset(sraw[:].bitcast(I32), 0)
        xsb = keep.tile([P, D], BF16, name="xsb", align_bytes=64)
        esc = keep.tile([P, 4], F32, name="esc")
        wraw = keep.tile([P, 1536], I32, name="wraw", align_bytes=64)
        g4 = keep.tile([P, 4], BF16, name="g4")
        w2w = keep.tile([P, O], I32, name="w2w", align_bytes=64)
        gam = keep.tile([P, O], BF16, name="gam")
        xt = keep.tile([P, 2, P], F32, name="xt", align_bytes=64)
        wper = keep.tile([P, 1536], I32, name="wper", align_bytes=64)
        sper = keep.tile([P, 1536], U8, name="sper", align_bytes=64)
        junk = keep.tile([P, O], BF16, name="junk", align_bytes=64)

        def do_L(c, k):
            t = fresh(eb, c, "eb", [P, TILES * D], U8, 6)
            nc.sync.dma_start(out=t[:], in_=e_rows[c])

        def do_C(c, k):
            t = fresh(ebf, c, "ebf", [P, TILES * D], BF16, 3)
            lo = k * 2 * D
            nc.scalar.copy(out=t[:, lo : lo + 2 * D], in_=eb[c][:, lo : lo + 2 * D].bitcast(FP8))

        def do_T(c, k):
            t = psum.tile([P, 2, 2 * P], F32, name="tr", tag="tr", bufs=2)
            words = ebf[c][:].bitcast(F32)
            for i in range(2):
                base = (2 * k + i) * (D // 2)
                for u in range(2):
                    nc.tensor.transpose(
                        t[:, u, i * P : (i + 1) * P], words[:, base + u : base + D // 2 : 2], ident[:]
                    )
            tr[c, k] = t

        def do_A(c, k):
            t = fresh(egr, c, "egr", [P, CHUNK * 4], BF16, 2)
            src = tr[c, k][:].rearrange("p u n -> p (u n)").bitcast(BF16)
            nc.vector.tensor_tensor(
                out=t[:, k * 1024 : (k + 1) * 1024].rearrange("p (n u e) -> p n u e", u=2, e=2),
                in0=src.rearrange("p (u n e) -> p n u e", u=2, e=2),
                in1=esc[:].rearrange("p (u e) -> p u e", e=2).unsqueeze(1).to_broadcast([P, 256, 2, 2]),
                op=ALU.mult,
            )

        def do_Q(c, k):
            t = fresh(ecod, c, "ecod", [P, CHUNK], U32, 2)
            q = fresh(escl, c, "escl", [P, CHUNK], U8, 2)
            nc.vector.quantize_mx(out=t[:].bitcast(FP8X4), scales=q[:], in_=egr[c][:])

        def do_M(c, k):
            t = psum.tile([P, 2, 2 * P], F32, name="hp", tag="hp", bufs=3)
            cols = slice(k // 2 * 256, (k // 2 + 1) * 256)
            b = c // CHUNKS_B
            scols = slice((c % 2) * P, (c % 2 + 1) * P)

            def add(dst, codes, scales, w0, j, start, stop):
                w = slice(w0 + j * P, w0 + (j + 1) * P)
                nc.tensor.matmul_mx(
                    out=dst,
                    lhsT=wper[:, w].bitcast(FP8X4),
                    lhsT_scale=sper[:, w],
                    rhs=codes.bitcast(FP8X4),
                    rhs_scale=scales,
                    start=start,
                    stop=stop,
                )

            for e in range(2):
                j = 2 * (k % 2) + e
                add(t[:, e, :], rcod[b][:, cols], rscl[b][:, cols], 1024, j, True, False)
                for i in range(2):
                    add(t[:, e, i * P : (i + 1) * P], scod[c // 2][:, scols], sscl[c // 2][:, scols], 512, j, False, False)
                add(t[:, e, :], ecod[c][:, cols], escl[c][:, cols], 0, j, False, True)
            hp[c, k] = t

        def do_S(c, k):
            t = fresh(hsil, c, "hsil", [P, CHUNK * 4], F32, 2)
            nc.scalar.activation(
                out=t[:, k * 512 : (k + 1) * 512].rearrange("p (n e) -> p n e", e=2),
                in_=hp[c, k][:].rearrange("p e n -> p n e"),
                func=ACT.Silu,
            )

        def do_F(c, k):
            t = fresh(hg, c, "hg", [P, CHUNK * 4], BF16, 3)
            cols = slice(k * 1024, (k + 1) * 1024)
            eng = nc.vector if (c, k) in ((0, 0),) else nc.gpsimd
            eng.tensor_tensor(
                out=t[:, cols].rearrange("p (n q e) -> p n q e", q=2, e=2),
                in0=hsil[c][:, cols].rearrange("p (q n e) -> p n q e", q=2, e=2),
                in1=gbig[:].rearrange("p (n q e) -> p n q e", q=2, e=2),
                op=ALU.mult,
            )

        def do_H(c, k):
            t = fresh(hcod, c, "hcod", [P, CHUNK], U32, 3)
            q = fresh(hscl, c, "hscl", [P, CHUNK], U8, 3)
            nc.vector.quantize_mx(out=t[:].bitcast(FP8X4), scales=q[:], in_=hg[c][:])

        def out_pass(dst, c, k, cols, start, stop):
            rows = slice(k * P, (k + 1) * P)
            nc.tensor.matmul_mx(
                out=dst,
                lhsT=hcod[c][:, rows].bitcast(FP8X4),
                lhsT_scale=hscl[c][:, rows],
                rhs=w2w[:, cols].bitcast(FP8X4),
                rhs_scale=sraw[:, 1536 + cols.start : 1536 + cols.stop],
                start=start,
                stop=stop,
            )

        def do_Y(c, k):
            yp[c, k] = psum.tile([P, O], F32, name="yp", tag="yp", bufs=3)
            out_pass(yp[c, k][:], c, k, slice(0, O), True, True)

        def do_B(c, k):
            nc.vector.bn_stats(out=stk[c % 3][:, k, 0:6], in_=yp[c, k][:])

        def do_G(c, k):
            t = fresh(mv, c, "mv", [P, TILES, 2], F32, 3)
            nc.vector.bn_aggr(out=t[:, k, :], in_=stk[c % 3][:, k, :])

        def center(c, k, scalar, op0):
            t = fresh(zs, c, "zs", [P, TILES, O], F32, 3)
            nc.vector.scalar_tensor_tensor(
                out=t[:, k, :], in0=yp[c, k][:], scalar=scalar, in1=gam[:], op0=op0, op1=ALU.mult
            )

        def do_E(c, k):
            center(c, k, mv[c][:, k, 0:1], ALU.subtract)

        def do_Z(c, k):
            t = psum.tile([P, 2, 2 * P], F32, name="hp", tag="hp", bufs=3)
            for i in range(4):
                out_pass(t[:, 0, 0:P], c, k - 5, slice(i * P, (i + 1) * P), i == 0, i == 3)
            ms[c, k - 5] = t

        def do_U(c, k):
            t = fresh(nmu, c, "nmu", [P, TILES], F32, 3)
            j = work.tile([P, P], BF16, name="ju", tag="ju", bufs=2)
            nc.scalar.activation(
                out=j[:], in_=ms[c, k - 5][:, 0, 0:P], func=ACT.Identity, scale=-1.0 / O, accum_out=t[:, k - 5 : k - 4]
            )

        def do_W(c, k):
            t = fresh(ssq, c, "ssq", [P, TILES], F32, 3)
            j = work.tile([P, O], BF16, name="jw", tag="jw", bufs=2)
            nc.scalar.activation(
                out=j[:], in_=yp[c, k][:], func=ACT.Square, bias=nmu[c][:, k : k + 1], accum_out=t[:, k : k + 1]
            )

        def do_J(c, k):
            t = fresh(mv, c, "mv", [P, TILES, 2], F32, 3)
            nc.scalar.activation(out=t[:, k, 1:2], in_=ssq[c][:, k : k + 1], func=ACT.Copy, scale=1.0 / O, bias=EPS)

        def do_Em(c, k):
            center(c, k, nmu[c][:, k : k + 1], ALU.add)

        def do_R(c, k):
            t = fresh(rstd, c, "rstd", [P, TILES], F32, 3)
            nc.gpsimd.tensor_tensor(out=t[:], in0=mv[c][:, :, 1], in1=mhalf[:], op=ALU.pow)

        def last_store(c, k):
            if c == CHUNKS - 1:
                nc.sync.dma_start(out=out_rows[c][:, k * O : (k + 1) * O], in_=res[c][:, k, :])

        def do_N(c, k):
            t = fresh(res, c, "res", [P, TILES, O], F32, 3)
            if c == CHUNKS - 1 and k == 2:
                nc.vector.tensor_scalar(
                    out=t[:, k, :], in0=zs[c][:, k, :], scalar1=rstd[c][:, k : k + 1], scalar2=None, op0=ALU.mult
                )
            else:
                nc.scalar.activation(out=t[:, k, :], in_=zs[c][:, k, :], func=ACT.Copy, scale=rstd[c][:, k : k + 1])
            last_store(c, k)

        def do_Ng(c, k):
            t = fresh(res, c, "res", [P, TILES, O], F32, 3)
            nc.gpsimd.tensor_scalar(
                out=t[:, k, :], in0=zs[c][:, k, :], scalar1=rstd[c][:, k : k + 1], scalar2=0.0, op0=ALU.mult, op1=ALU.add
            )
            last_store(c, k)

        def do_O(c, k):
            if c < CHUNKS - 1:
                nc.sync.dma_start(out=out_rows[c], in_=res[c][:].rearrange("p r o -> p (r o)"))

        def send_copy(q):
            t = fresh(sgr, q, "sgr", [P, 16 * REP * 4], BF16, 2)
            eng = nc.vector if q == 0 else nc.gpsimd
            eng.tensor_copy(
                out=t[:].bitcast(I32).rearrange("p (i r u) -> p i r u", i=16, u=2),
                in_=xt[:].rearrange("p u n -> p (u n)").bitcast(I32)
                .rearrange("p (u n) -> p u n", u=2)[:, :, 16 * q : 16 * q + 16]
                .rearrange("p u i -> p i u")
                .unsqueeze(2)
                .to_broadcast([P, 16, REP, 2]),
            )

        def send_quant(q):
            t = fresh(scod, q, "scod", [P, 16 * REP], U32, 2)
            v = fresh(sscl, q, "sscl", [P, 16 * REP], U8, 2)
            nc.vector.quantize_mx(out=t[:].bitcast(FP8X4), scales=v[:], in_=sgr[q][:])

        def recv_copy(b):
            t = fresh(rgr, b, "rgr", [P, TILES * P * 4], BF16, 1)
            for k in range(TILES):
                nc.scalar.copy(
                    out=t[:, k * 512 : (k + 1) * 512].bitcast(F32).rearrange("p (r j u) -> p r j u", r=SENDERS, u=2),
                    in_=xt[:, :, b * N + k : (b + 1) * N : TILES]
                    .rearrange("p u j -> p j u")
                    .unsqueeze(1)
                    .to_broadcast([P, SENDERS, N // TILES, 2]),
                )

        def recv_quant(b):
            t = fresh(rcod, b, "rcod", [P, TILES * P], U32, 2)
            v = fresh(rscl, b, "rscl", [P, TILES * P], U8, 2)
            nc.vector.quantize_mx(out=t[:].bitcast(FP8X4), scales=v[:], in_=rgr[b][:])

        def permute():
            for dst, raw in ((wper, wraw), (sper, sraw)):
                nc.vector.tensor_copy(
                    out=dst[:].rearrange("p (w t m) -> p w t m", w=3, t=4),
                    in_=raw[:, 0:1536].rearrange("p (w m t) -> p w t m", w=3, t=4),
                )

        def scale_rows(src, lo, n):
            view = src[0].rearrange("(q r) n -> r q n", r=4)
            for r in range(4):
                nc.sync.dma_start(out=sraw[r:P:32, lo : lo + n].bitcast(I32), in_=view[r].bitcast(I32))

        def once(s):
            if s == -5:
                nc.sync.dma_start(out=xsb[:], in_=x.rearrange("b i k -> (b i) k"))
                nc.sync.dma_start(out=esc[:], in_=e_scale.rearrange("a b c (p t) -> p (a b c t)", t=4))
                scale_rows(wn_scales, 512, 1024)
                nc.sync.dma_start(out=wraw[:, 512:1536], in_=wn_words[0].rearrange("p n t -> p (n t)").bitcast(I32))
                scale_rows(we_scales, 0, 512)
                nc.sync.dma_start(out=wraw[:, 0:512], in_=we_words[0].rearrange("p n t -> p (n t)").bitcast(I32))
                nc.sync.dma_start(out=g4[:], in_=g.rearrange("(p t) -> p t", t=4))
                xtp = psum.tile([P, 2, P], F32, name="xtp", tag="yp", bufs=3)
                for u in range(2):
                    nc.tensor.transpose(xtp[:, u, :], xsb[:].bitcast(F32)[:, u : D // 2 : 2], ident[:])
                nc.vector.tensor_copy(out=xt[:], in_=xtp[:])
                send_copy(0)
                send_quant(0)
                permute()
                nc.gpsimd.tensor_copy(
                    out=gbig[:].rearrange("p (n t) -> p n t", t=4), in_=g4[:].unsqueeze(1).to_broadcast([P, 256, 4])
                )
            if s == -4:
                scale_rows(w2_scales, 1536, 512)
                nc.sync.dma_start(out=w2w[:], in_=w2_words[0].rearrange("p n t -> p (n t)").bitcast(I32))
                nc.sync.dma_start(out=gam[:], in_=gamma.partition_broadcast(P))
            if s == -1:
                recv_copy(0)
                recv_quant(0)
            if s >= 0 and s % 2 == 0 and s + 2 < CHUNKS:
                send_copy(s // 2 + 1)
            if s >= 0 and s % 2 == 1 and s + 1 < CHUNKS:
                send_quant((s + 1) // 2)
            if s == CHUNKS_B - 3:
                recv_copy(1)
            if s == CHUNKS_B - 2:
                recv_quant(1)

        steps = {
            "C": do_C,
            "A": do_A,
            "Y": do_Y,
            "Z": do_Z,
            "B": do_B,
            "M": do_M,
            "U": do_U,
            "G": do_G,
            "Em": do_Em,
            "E": do_E,
            "N": do_N,
            "S": do_S,
            "L": do_L,
            "H": do_H,
            "Q": do_Q,
            "W": do_W,
            "J": do_J,
            "F": do_F,
            "T": do_T,
            "R": do_R,
            "O": do_O,
        }
        for s in range(-5, CHUNKS + 4):
            for op, k, lag, par in PROGRAM:
                if 0 <= s - lag < CHUNKS and (s - lag) % 2 in par:
                    steps[op](s - lag, k)
            once(s)
